import numpy as np
import ml_dtypes


def mxq(x, axis, fmt="e4m3"):
    dtype, down = {"e4m3": (ml_dtypes.float8_e4m3fn, 7), "e5m2": (ml_dtypes.float8_e5m2, 14)}[fmt]
    v = np.moveaxis(np.asarray(x, np.float32).astype(ml_dtypes.bfloat16).astype(np.float64), axis, -1)
    blocks = v.reshape(v.shape[:-1] + (-1, 32))
    amax = np.abs(blocks).max(-1, keepdims=True)
    byte = np.maximum(np.where(amax > 0, np.frexp(amax)[1] - 1 + 127, 0) - down, 1)
    scale = np.exp2(byte - 127.0)
    codes = (blocks / scale).astype(np.float32).astype(dtype).astype(np.float64)
    return np.moveaxis((codes * scale).reshape(v.shape), -1, axis)


WIDE = False


def mx_kscale(k):
    if not WIDE:
        return np.ones(k)
    levels = np.array([10, -10, 5, -5, 0])
    if k % 512:
        return np.exp2(np.random.permutation(np.resize(levels, k // 32))).repeat(32)
    a = np.empty((k // 512, 16))
    for p in range(k // 512):
        a[p, :8] = np.random.permutation(np.resize(levels, 8))
        for g in range(8):
            far = levels[np.abs(levels - a[p, g]) >= 10]
            a[p, g + 8] = far[np.random.randint(len(far))]
    return np.exp2(a.ravel()).repeat(32)


def f64(x):
    return np.asarray(x).astype(np.float64)


def striped(idx):
    return np.tile(np.asarray(idx).reshape(-1, 16).T, (8, 1)).astype(np.uint16)


def unstriped(offs):
    return offs[:16].T.reshape(-1).astype(np.int64)


E2M1 = np.array([0.0, 0.5, 1.0, 1.5, 2.0, 3.0, 4.0, 6.0, -0.0, -0.5, -1.0, -1.5, -2.0, -3.0, -4.0, -6.0])


def pack_weight(w, fmt):
    k, n = w.shape
    w = f64(np.asarray(w, np.float32).astype(ml_dtypes.bfloat16)).reshape(k // 32, 32, n)
    amax = np.abs(w).max(1)
    if fmt == "e4m3":
        byte = np.frexp(amax)[1] - 1 + 127 - 7
    else:
        mant, ex = np.frexp(amax / 6.0)
        byte = np.where(mant > 0.5, ex, ex - 1) + 127
    byte = np.clip(np.where(amax > 0, byte, 1), 1, 254)
    scaled = (w * np.exp2(127.0 - byte)[:, None, :]).reshape(k, n).astype(np.float32)
    by_word = np.ascontiguousarray(scaled.reshape(k // 512, 128, 4, n).transpose(0, 1, 3, 2))
    if fmt == "e4m3":
        words = by_word.astype(ml_dtypes.float8_e4m3fn).view(np.uint8)
    else:
        c = by_word.astype(ml_dtypes.float4_e2m1fn).view(np.uint8) & 0xF
        words = (c[..., 0::2] | (c[..., 1::2] << 4)).reshape(k // 512, 128, 2 * n)
    return np.ascontiguousarray(words), np.ascontiguousarray(byte.astype(np.uint8).reshape(k // 512, 16, n))


def unpack_weight(words, scales, fmt):
    g, _, n = scales.shape
    words = np.ascontiguousarray(words).reshape(g, 128, n, -1)
    if fmt == "e4m3":
        vals = words.view(ml_dtypes.float8_e4m3fn).astype(np.float64)
    else:
        nib = np.empty((g, 128, n, 4), np.uint8)
        nib[..., 0::2] = words & 0xF
        nib[..., 1::2] = words >> 4
        vals = E2M1[nib]
    vals = vals * np.repeat(np.exp2(scales.astype(np.float64) - 127.0), 8, axis=1)[..., None]
    return vals.transpose(0, 1, 3, 2).reshape(g * 512, n)


B, N, T, D, NQ = 1, 512, 2048, 512, 512
DV = 512


def sgn(shape):
    return np.random.uniform(0.5, 2.0, shape) * np.where(np.random.standard_normal(shape) < 0, -1.0, 1.0)


def setup_inputs():
    n = np.random.standard_normal
    idx = np.random.permutation(T)[:B * N]
    idx2 = np.random.permutation(1024)[:B * N]
    s = mx_kscale(D)[:, None]
    u = mx_kscale(N)
    ut = np.ones(T)
    ut[idx] = u
    kp = pack_weight(n((D, T)) / s, "e4m3")
    cp = pack_weight(n((D, 1024)) / s, "e4m3")
    return {
        "uT": (n((B, D, NQ)) * s * (0.50 / np.sqrt(D))).astype(np.float32),
        "pT": (n((B, D, NQ)) * s * (0.50 / np.sqrt(D))).astype(np.float32),
        "k_words": kp[0],
        "k_scales": kp[1],
        "c_words": cp[0],
        "c_scales": cp[1],
        "vT": (n((DV, T)) / ut).astype(np.float32),
        "ls": (np.random.uniform(7.0, 7.6, (B, 1, NQ))).astype(np.float32),
        "us": (sgn((B, N, 1)) * u[:, None]).astype(np.float32),
        "offs": striped(idx),
        "offs2": striped(idx2),
    }


def reference(uT, pT, k_words, k_scales, c_words, c_scales, vT, ls, us, offs, offs2):
    idx = unstriped(offs)
    idx2 = unstriped(offs2)
    pick = lambda x, which: x[:, which].reshape(x.shape[0], B, -1).transpose(1, 0, 2)
    k = unpack_weight(k_words, k_scales, "e4m3")
    kg = pick(k, idx)
    c = unpack_weight(c_words, c_scales, "e4m3")
    cg = pick(c, idx2)
    uq = mxq(f64(uT), 1, "e4m3")
    pq = mxq(f64(pT), 1, "e4m3")
    a = (kg.transpose(0, 2, 1) @ uq) + (cg.transpose(0, 2, 1) @ pq)
    y = np.exp(a - f64(ls)) * f64(us)
    wq = mxq(y, 1, "e4m3")
    o = wq.transpose(0, 2, 1) @ mxq(pick(f64(vT), idx).transpose(0, 2, 1), 1, "e4m3")
    return o

@@ -1,0 +1,201 @@
+from contextlib import ExitStack
+
+import concourse.mybir as mybir
+from concourse.masks import make_identity
+
+F32 = mybir.dt.float32
+BF16 = mybir.dt.bfloat16
+I32 = mybir.dt.int32
+U32 = mybir.dt.uint32
+U16 = mybir.dt.uint16
+U8 = mybir.dt.uint8
+FP8X4 = mybir.dt.float8_e4m3fn_x4
+
+P = 128
+PACK = 4
+SLOTS = 512
+TOKENS = 2048
+DISTANCES = 1024
+QUERIES = 512
+VALUES = 512
+Q_BLOCKS = QUERIES // P
+V_BLOCKS = VALUES // P
+C_PLANE = 4
+
+FLOPS = 3 * 2 * 512 * 512 * 512
+
+
+def tile_attend_at_txl_topk_kernel(tc, uT, pT, k_words, k_scales, c_words, c_scales, vT, ls, us, offs, offs2, out):
+    nc = tc.nc
+    with ExitStack() as ctx:
+        keep = ctx.enter_context(tc.tile_pool(name="keep", bufs=1))
+        ring = ctx.enter_context(tc.tile_pool(name="ring", bufs=2))
+        psum = ctx.enter_context(tc.psum_pool(name="psum", bufs=1))
+
+        tok_list = keep.tile([P, SLOTS // 16], U16, name="tok_list")
+        dist_list = keep.tile([P, SLOTS // 16], U16, name="dist_list")
+        c_word_pool = keep.tile([P, DISTANCES], I32, name="c_word_pool")
+        k_word_pool = keep.tile([P, TOKENS], I32, name="k_word_pool")
+        c_byte_pool = keep.tile([P, DISTANCES // 4], I32, name="c_byte_pool")
+        k_byte_pool = keep.tile([P, TOKENS // 4], I32, name="k_byte_pool")
+        u_raw = keep.tile([P, PACK, QUERIES], F32, name="u_raw")
+        p_raw = keep.tile([P, PACK, QUERIES], F32, name="p_raw")
+        v_pool = [keep.tile([P, TOKENS], F32, name="v_pool%d" % b) for b in range(V_BLOCKS)]
+        ls_rows = keep.tile([P, P], F32, name="ls_rows")
+        us_cols = keep.tile([P, PACK], F32, name="us_cols")
+        ident = keep.tile([P, P], F32, name="ident")
+        neg_ls = keep.tile([P, Q_BLOCKS], F32, name="neg_ls")
+
+        nc.vector.memset(c_byte_pool[:], 0)
+        nc.vector.memset(k_byte_pool[:], 0)
+        nc.gpsimd.memset(ls_rows[:], 0.0)
+        make_identity(nc, ident[:])
+
+        def load_scale_rows(pool_tile, rows, first):
+            rows = rows[0].bitcast(I32)
+            for r in range(4):
+                nc.sync.dma_start(pool_tile[first + r : P : 32, :], rows[r:16:4, :])
+
+        def words_of(x):
+            return x[0].rearrange("p n t -> p (n t)").bitcast(I32)
+
+        nc.sync.dma_start(dist_list[:], offs2)
+        nc.sync.dma_start(c_word_pool[:], words_of(c_words))
+        load_scale_rows(c_byte_pool, c_scales, C_PLANE)
+        nc.sync.dma_start(k_word_pool[:], words_of(k_words))
+        nc.sync.dma_start(tok_list[:], offs)
+        load_scale_rows(k_byte_pool, k_scales, 0)
+        nc.sync.dma_start(u_raw[:], uT[0].rearrange("(p t) q -> p t q", t=PACK))
+        nc.sync.dma_start(ls_rows[0:Q_BLOCKS, :], ls[0].rearrange("o (b m) -> (o b) m", m=P))
+        nc.sync.dma_start(p_raw[:], pT[0].rearrange("(p t) q -> p t q", t=PACK))
+        nc.sync.dma_start(us_cols[:], us[0].rearrange("(p t) o -> p (t o)", t=PACK))
+        for b in range(V_BLOCKS):
+            nc.sync.dma_start(v_pool[b][:], vT[b * P : (b + 1) * P, :])
+
+        c_codes = keep.tile([P, SLOTS], U32, name="c_codes", align_bytes=64)
+        c_bytes = keep.tile([P, SLOTS], U8, name="c_bytes", align_bytes=64)
+        k_codes = keep.tile([P, SLOTS], U32, name="k_codes", align_bytes=64)
+        k_bytes = keep.tile([P, SLOTS], U8, name="k_bytes", align_bytes=64)
+        nc.vector.tensor_copy(c_codes[:], c_word_pool[:].bitcast(U32).indirect(dist_list[:]))
+        nc.vector.tensor_copy(c_bytes[:], c_byte_pool[:].bitcast(U8).indirect(dist_list[:]))
+        nc.vector.tensor_copy(k_codes[:], k_word_pool[:].bitcast(U32).indirect(tok_list[:]))
+        nc.vector.tensor_copy(k_bytes[:], k_byte_pool[:].bitcast(U8).indirect(tok_list[:]))
+
+        def interleave(copy, grouped, raw, qb):
+            src = raw[:, :, qb * P : (qb + 1) * P].rearrange("p t (c i) -> p c t i", i=4)
+            copy(grouped.rearrange("p (c i t) -> p c t i", i=4, t=PACK), src)
+
+        def quantize(name, grouped):
+            width = grouped.shape[1] // PACK
+            codes = keep.tile([P, width], U32, name=name + "_codes", align_bytes=64)
+            scales = keep.tile([P, width], U8, name=name + "_scales", align_bytes=64)
+            nc.vector.quantize_mx(out=codes[:].bitcast(FP8X4), scales=scales[:], in_=grouped)
+            return codes, scales
+
+        ls_turn = psum.tile([P, PACK, P], F32, name="turn", bufs=2)
+        nc.tensor.transpose(ls_turn[:, 0, :], ls_rows[:], ident[:])
+        nc.scalar.mul(neg_ls[:], ls_turn[:, 0, 0:Q_BLOCKS], -1.0)
+
+        u_grouped = keep.tile([P, QUERIES * PACK], BF16, name="u_grouped", align_bytes=64)
+        for qb in range(Q_BLOCKS):
+            copy = nc.scalar.copy if qb == Q_BLOCKS - 1 else nc.vector.tensor_copy
+            interleave(copy, u_grouped[:, qb * 512 : (qb + 1) * 512], u_raw, qb)
+        u_codes, u_scales = quantize("u", u_grouped[:])
+
+        scores = [psum.tile([P, SLOTS], F32, name="score%d" % qb) for qb in range(Q_BLOCKS)]
+        for qb in range(Q_BLOCKS):
+            cols = slice(qb * P, (qb + 1) * P)
+            nc.tensor.matmul_mx(
+                out=scores[qb][:], lhsT=u_codes[:, cols].bitcast(FP8X4), lhsT_scale=u_scales[:, cols],
+                rhs=k_codes[:].bitcast(FP8X4), rhs_scale=k_bytes[:], start=True, stop=False,
+            )
+
+        p_grouped = [keep.tile([P, P * PACK], BF16, name="p_grouped%d" % qb, align_bytes=64) for qb in range(Q_BLOCKS)]
+        weights = [keep.tile([P, PACK, P], F32, name="weights%d" % qb) for qb in range(Q_BLOCKS)]
+
+        def position_pass(qb):
+            codes, scales = quantize("p%d" % qb, p_grouped[qb][:])
+            nc.tensor.matmul_mx(
+                out=scores[qb][:], lhsT=codes[:].bitcast(FP8X4), lhsT_scale=scales[:],
+                rhs=c_codes[:].bitcast(FP8X4), rhs_scale=c_bytes[C_PLANE:P, :], start=False, stop=True,
+            )
+            nc.scalar.activation(
+                weights[qb][:], scores[qb][:].rearrange("q (p t) -> q t p", t=PACK),
+                mybir.ActivationFunctionType.Exp, bias=neg_ls[:, qb : qb + 1],
+            )
+
+        for qb in range(Q_BLOCKS):
+            interleave(nc.scalar.copy if qb % 2 else nc.vector.tensor_copy, p_grouped[qb][:], p_raw, qb)
+        for qb in range(Q_BLOCKS):
+            position_pass(qb)
+
+        us_wide = us_cols[:].unsqueeze(1).to_broadcast([P, P, PACK])
+        y_grouped = [keep.tile([P, P, PACK], BF16, name="y_grouped%d" % qb, align_bytes=64) for qb in range(Q_BLOCKS)]
+        y_mx = [None] * Q_BLOCKS
+        v_mx = [None] * V_BLOCKS
+        v_grouped = [keep.tile([P, P * PACK], BF16, name="v_grouped%d" % b, align_bytes=64) for b in range(V_BLOCKS)]
+
+        def weigh(qb):
+            turned = psum.tile([P, PACK, P], F32, name="turn", bufs=2)
+            for t in range(PACK):
+                nc.tensor.transpose(turned[:, t, :], weights[qb][:, t, :], ident[:])
+            nc.vector.tensor_tensor(
+                y_grouped[qb][:], turned[:].rearrange("p t q -> p q t"), us_wide, mybir.AluOpType.mult
+            )
+
+        def quantize_y(qb):
+            y_mx[qb] = quantize("y%d" % qb, y_grouped[qb][:].rearrange("p q t -> p (q t)"))
+
+        def gather_values(b):
+            picked = ring.tile([P, 2, P, 2], BF16, name="picked")
+            nc.vector.tensor_copy(picked[:].rearrange("e u p j -> e p u j"), v_pool[b][:].indirect(tok_list[:]))
+            pairs = picked[:].rearrange("e u p j -> e (u p j)").bitcast(F32)
+            turned = psum.tile([P, PACK, P], F32, name="v_turn", bufs=2)
+            for u in range(2):
+                nc.tensor.transpose(turned[:, u, :], pairs[:, u * P : (u + 1) * P], ident[:])
+            nc.scalar.copy(
+                v_grouped[b][:].bitcast(F32).rearrange("p (e u) -> p e u", u=2),
+                turned[:, 0:2, :].rearrange("p u e -> p e u"),
+            )
+
+        def quantize_v(b):
+            v_mx[b] = quantize("v%d" % b, v_grouped[b][:])
+
+        out_rows = out[0].rearrange("(b q) e -> q b e", q=P)
+
+        def product(b, q_blocks, copy, staged, bank):
+            acc = psum.tile([P, Q_BLOCKS, P], F32, name="score%d" % bank)
+            for i, qb in enumerate(q_blocks):
+                nc.tensor.matmul_mx(
+                    out=acc[:, i, :], lhsT=y_mx[qb][0][:].bitcast(FP8X4), lhsT_scale=y_mx[qb][1][:],
+                    rhs=v_mx[b][0][:].bitcast(FP8X4), rhs_scale=v_mx[b][1][:], start=True, stop=True,
+                )
+            copy(staged, acc[:, 0 : len(q_blocks), :])
+
+        gather_values(0)
+        weigh(0)
+        weigh(1)
+        quantize_v(0)
+        quantize_y(0)
+        weigh(2)
+        quantize_y(1)
+        weigh(3)
+        quantize_y(2)
+        gather_values(1)
+        quantize_y(3)
+        quantize_v(1)
+        front = keep.tile([P, Q_BLOCKS, 2 * P], F32, name="front")
+        product(0, range(4), nc.scalar.copy, front[:, :, 0:P], 0)
+        product(1, range(4), nc.scalar.copy, front[:, :, P : 2 * P], 1)
+        nc.sync.dma_start(out_rows[:, :, 0 : 2 * P], front[:])
+        gather_values(2)
+        quantize_v(2)
+        third = keep.tile([P, Q_BLOCKS, P], F32, name="third")
+        product(2, range(4), nc.scalar.copy, third[:], 2)
+        nc.sync.dma_start(out_rows[:, :, 2 * P : 3 * P], third[:])
+        gather_values(3)
+        quantize_v(3)
+        for half, copy in enumerate((nc.scalar.copy, nc.vector.tensor_copy)):
+            last = keep.tile([P, 2, P], F32, name="last%d" % half)
+            product(3, range(2 * half, 2 * half + 2), copy, last[:], 3 * (1 - half))
+            nc.sync.dma_start(out_rows[:, 2 * half : 2 * half + 2, 3 * P : 4 * P], last[:])

@@ -29,7 +29,6 @@ def tile_attend_at_txl_topk_kernel(tc, uT, pT, k_words, k_scales, c_words, c_sca
     nc = tc.nc
     with ExitStack() as ctx:
         keep = ctx.enter_context(tc.tile_pool(name="keep", bufs=1))
-        ring = ctx.enter_context(tc.tile_pool(name="ring", bufs=2))
         psum = ctx.enter_context(tc.psum_pool(name="psum", bufs=1))
 
         tok_list = keep.tile([P, SLOTS // 16], U16, name="tok_list")
@@ -39,15 +38,15 @@ def tile_attend_at_txl_topk_kernel(tc, uT, pT, k_words, k_scales, c_words, c_sca
         c_byte_pool = keep.tile([P, DISTANCES // 4], I32, name="c_byte_pool")
         k_byte_pool = keep.tile([P, TOKENS // 4], I32, name="k_byte_pool")
         u_raw = keep.tile([P, PACK, QUERIES], F32, name="u_raw")
-        p_raw = keep.tile([P, PACK, QUERIES], F32, name="p_raw")
-        v_pool = [keep.tile([P, TOKENS], F32, name="v_pool%d" % b) for b in range(V_BLOCKS)]
+        p_raw = [keep.tile([P, PACK, QUERIES // 2], F32, name="p_raw%d" % h) for h in range(2)]
+        v_pool = [keep.tile([P, TOKENS], F32, name="v_pool%d" % b, align_bytes=64) for b in range(V_BLOCKS)]
         ls_rows = keep.tile([P, P], F32, name="ls_rows")
         us_cols = keep.tile([P, PACK], F32, name="us_cols")
         ident = keep.tile([P, P], F32, name="ident")
         neg_ls = keep.tile([P, Q_BLOCKS], F32, name="neg_ls")
 
-        nc.vector.memset(c_byte_pool[:], 0)
-        nc.vector.memset(k_byte_pool[:], 0)
+        nc.gpsimd.memset(c_byte_pool[:], 0)
+        nc.gpsimd.memset(k_byte_pool[:], 0)
         nc.gpsimd.memset(ls_rows[:], 0.0)
         make_identity(nc, ident[:])
 
@@ -66,9 +65,10 @@ def tile_attend_at_txl_topk_kernel(tc, uT, pT, k_words, k_scales, c_words, c_sca
         nc.sync.dma_start(tok_list[:], offs)
         load_scale_rows(k_byte_pool, k_scales, 0)
         nc.sync.dma_start(u_raw[:], uT[0].rearrange("(p t) q -> p t q", t=PACK))
-        nc.sync.dma_start(ls_rows[0:Q_BLOCKS, :], ls[0].rearrange("o (b m) -> (o b) m", m=P))
-        nc.sync.dma_start(p_raw[:], pT[0].rearrange("(p t) q -> p t q", t=PACK))
-        nc.sync.dma_start(us_cols[:], us[0].rearrange("(p t) o -> p (t o)", t=PACK))
+        for h in range(2):
+            nc.sync.dma_start(p_raw[h][:], pT[0].rearrange("(p t) q -> p t q", t=PACK)[:, :, h * 256 : (h + 1) * 256])
+        nc.gpsimd.dma_start(ls_rows[0:Q_BLOCKS, :], ls[0].rearrange("o (b m) -> (o b) m", m=P))
+        nc.gpsimd.dma_start(us_cols[:], us[0].rearrange("(p t) o -> p (t o)", t=PACK))
         for b in range(V_BLOCKS):
             nc.sync.dma_start(v_pool[b][:], vT[b * P : (b + 1) * P, :])
 
@@ -81,121 +81,142 @@ def tile_attend_at_txl_topk_kernel(tc, uT, pT, k_words, k_scales, c_words, c_sca
         nc.vector.tensor_copy(k_codes[:], k_word_pool[:].bitcast(U32).indirect(tok_list[:]))
         nc.vector.tensor_copy(k_bytes[:], k_byte_pool[:].bitcast(U8).indirect(tok_list[:]))
 
-        def interleave(copy, grouped, raw, qb):
-            src = raw[:, :, qb * P : (qb + 1) * P].rearrange("p t (c i) -> p c t i", i=4)
+        def interleave(copy, grouped, raw):
+            src = raw.rearrange("p t (c i) -> p c t i", i=4)
             copy(grouped.rearrange("p (c i t) -> p c t i", i=4, t=PACK), src)
 
-        def quantize(name, grouped):
-            width = grouped.shape[1] // PACK
-            codes = keep.tile([P, width], U32, name=name + "_codes", align_bytes=64)
-            scales = keep.tile([P, width], U8, name=name + "_scales", align_bytes=64)
-            nc.vector.quantize_mx(out=codes[:].bitcast(FP8X4), scales=scales[:], in_=grouped)
+        def code_tile(name, width, slot=""):
+            return keep.tile([P, width], U32, name=name + "_codes", tag=slot, align_bytes=64)
+
+        def quantize(name, grouped, codes):
+            scales = keep.tile([P, codes.shape[1]], U8, name=name + "_scales", align_bytes=64)
+            nc.vector.quantize_mx(out=codes.bitcast(FP8X4), scales=scales[:], in_=grouped)
             return codes, scales
 
         ls_turn = psum.tile([P, PACK, P], F32, name="turn", bufs=2)
         nc.tensor.transpose(ls_turn[:, 0, :], ls_rows[:], ident[:])
         nc.scalar.mul(neg_ls[:], ls_turn[:, 0, 0:Q_BLOCKS], -1.0)
 
-        u_grouped = keep.tile([P, QUERIES * PACK], BF16, name="u_grouped", align_bytes=64)
-        for qb in range(Q_BLOCKS):
-            copy = nc.scalar.copy if qb == Q_BLOCKS - 1 else nc.vector.tensor_copy
-            interleave(copy, u_grouped[:, qb * 512 : (qb + 1) * 512], u_raw, qb)
-        u_codes, u_scales = quantize("u", u_grouped[:])
-
+        halves = range(2)
+        u_grouped = [keep.tile([P, 2 * P * PACK], BF16, name="u_grouped%d" % h, align_bytes=64) for h in halves]
+        p_grouped = [keep.tile([P, 2 * P * PACK], BF16, name="p_grouped%d" % h, align_bytes=64) for h in halves]
         scores = [psum.tile([P, SLOTS], F32, name="score%d" % qb) for qb in range(Q_BLOCKS)]
+
+        def score_pass(qb, mx, codes, plane, first):
+            cols = slice(qb % 2 * P, (qb % 2 + 1) * P)
+            nc.tensor.matmul_mx(
+                out=scores[qb][:], lhsT=mx[0][:, cols].bitcast(FP8X4), lhsT_scale=mx[1][:, cols],
+                rhs=codes[:].bitcast(FP8X4), rhs_scale=plane, start=first, stop=not first,
+            )
+
+        def content_passes(h, slot):
+            u_mx = quantize("u%d" % h, u_grouped[h][:], code_tile("u%d" % h, 256, slot)[:])
+            for qb in (2 * h, 2 * h + 1):
+                score_pass(qb, u_mx, k_codes, k_bytes[:], True)
+
+        def position_passes(h):
+            interleave(nc.scalar.copy, p_grouped[h][:, 0:512], p_raw[h][:, :, 0:P])
+            interleave(nc.vector.tensor_copy, p_grouped[h][:, 512:1024], p_raw[h][:, :, P : 2 * P])
+            p_mx = quantize("p%d" % h, p_grouped[h][:], code_tile("p%d" % h, 256)[:])
+            for qb in (2 * h, 2 * h + 1):
+                score_pass(qb, p_mx, c_codes, c_bytes[C_PLANE:P, :], False)
+
+        interleave(nc.vector.tensor_copy, u_grouped[0][:], u_raw[:, :, 0:256])
+        interleave(nc.scalar.copy, u_grouped[1][:], u_raw[:, :, 256:512])
+        content_passes(0, "")
+        position_passes(0)
+        content_passes(1, "p_grouped0")
+        position_passes(1)
+        weight_tile = keep.tile([P, Q_BLOCKS, PACK, P], F32, name="weights", tag="p_grouped1", align_bytes=64)
+        weights = [weight_tile[:, qb] for qb in range(Q_BLOCKS)]
         for qb in range(Q_BLOCKS):
-            cols = slice(qb * P, (qb + 1) * P)
-            nc.tensor.matmul_mx(
-                out=scores[qb][:], lhsT=u_codes[:, cols].bitcast(FP8X4), lhsT_scale=u_scales[:, cols],
-                rhs=k_codes[:].bitcast(FP8X4), rhs_scale=k_bytes[:], start=True, stop=False,
-            )
-
-        p_grouped = [keep.tile([P, P * PACK], BF16, name="p_grouped%d" % qb, align_bytes=64) for qb in range(Q_BLOCKS)]
-        weights = [keep.tile([P, PACK, P], F32, name="weights%d" % qb) for qb in range(Q_BLOCKS)]
-
-        def position_pass(qb):
-            codes, scales = quantize("p%d" % qb, p_grouped[qb][:])
-            nc.tensor.matmul_mx(
-                out=scores[qb][:], lhsT=codes[:].bitcast(FP8X4), lhsT_scale=scales[:],
-                rhs=c_codes[:].bitcast(FP8X4), rhs_scale=c_bytes[C_PLANE:P, :], start=False, stop=True,
-            )
             nc.scalar.activation(
-                weights[qb][:], scores[qb][:].rearrange("q (p t) -> q t p", t=PACK),
+                weights[qb], scores[qb][:].rearrange("q (p t) -> q t p", t=PACK),
                 mybir.ActivationFunctionType.Exp, bias=neg_ls[:, qb : qb + 1],
             )
 
-        for qb in range(Q_BLOCKS):
-            interleave(nc.scalar.copy if qb % 2 else nc.vector.tensor_copy, p_grouped[qb][:], p_raw, qb)
-        for qb in range(Q_BLOCKS):
-            position_pass(qb)
-
         us_wide = us_cols[:].unsqueeze(1).to_broadcast([P, P, PACK])
-        y_grouped = [keep.tile([P, P, PACK], BF16, name="y_grouped%d" % qb, align_bytes=64) for qb in range(Q_BLOCKS)]
-        y_mx = [None] * Q_BLOCKS
-        v_mx = [None] * V_BLOCKS
-        v_grouped = [keep.tile([P, P * PACK], BF16, name="v_grouped%d" % b, align_bytes=64) for b in range(V_BLOCKS)]
+        y_grouped = [
+            keep.tile([P, 2, P, PACK], BF16, name="y_grouped%d" % h, tag=("v_pool0", "")[h], align_bytes=64)
+            for h in halves
+        ]
+        picked = [keep.tile([P, 2, P, 2], BF16, name="picked%d" % b) for b in range(V_BLOCKS)]
+        v_grouped = keep.tile([P, V_BLOCKS, P * PACK], BF16, name="v_grouped", align_bytes=64)
 
-        def weigh(qb):
-            turned = psum.tile([P, PACK, P], F32, name="turn", bufs=2)
+        def turn_weights(qb, turned):
             for t in range(PACK):
                 nc.tensor.transpose(turned[:, t, :], weights[qb][:, t, :], ident[:])
+            return turned
+
+        def scale_on_vector(qb):
+            turned = turn_weights(qb, psum.tile([P, PACK, P], F32, name="turn", bufs=2))
             nc.vector.tensor_tensor(
-                y_grouped[qb][:], turned[:].rearrange("p t q -> p q t"), us_wide, mybir.AluOpType.mult
+                y_grouped[0][:, qb], turned[:].rearrange("p t q -> p q t"), us_wide, mybir.AluOpType.mult
             )
 
-        def quantize_y(qb):
-            y_mx[qb] = quantize("y%d" % qb, y_grouped[qb][:].rearrange("p q t -> p (q t)"))
+        def scale_on_scalar(qb):
+            turned = turn_weights(qb, psum.tile([P, PACK, P], F32, name="score%d" % (qb - 2)))
+            for t in range(PACK):
+                nc.scalar.activation(
+                    y_grouped[1][:, qb - 2, :, t], turned[:, t, :],
+                    mybir.ActivationFunctionType.Copy, scale=us_cols[:, t : t + 1],
+                )
+
+        def quantize_y(h, codes):
+            return quantize("y%d" % h, y_grouped[h][:].rearrange("p b q t -> p (b q t)"), codes)
 
         def gather_values(b):
-            picked = ring.tile([P, 2, P, 2], BF16, name="picked")
-            nc.vector.tensor_copy(picked[:].rearrange("e u p j -> e p u j"), v_pool[b][:].indirect(tok_list[:]))
-            pairs = picked[:].rearrange("e u p j -> e (u p j)").bitcast(F32)
+            nc.vector.tensor_copy(picked[b][:].rearrange("e u p j -> e p u j"), v_pool[b][:].indirect(tok_list[:]))
+
+        def turn_values(b, copy):
+            pairs = picked[b][:].rearrange("e u p j -> e (u p j)").bitcast(F32)
             turned = psum.tile([P, PACK, P], F32, name="v_turn", bufs=2)
             for u in range(2):
                 nc.tensor.transpose(turned[:, u, :], pairs[:, u * P : (u + 1) * P], ident[:])
-            nc.scalar.copy(
-                v_grouped[b][:].bitcast(F32).rearrange("p (e u) -> p e u", u=2),
+            copy(
+                v_grouped[:, b].bitcast(F32).rearrange("p (e u) -> p e u", u=2),
                 turned[:, 0:2, :].rearrange("p u e -> p e u"),
             )
 
-        def quantize_v(b):
-            v_mx[b] = quantize("v%d" % b, v_grouped[b][:])
-
         out_rows = out[0].rearrange("(b q) e -> q b e", q=P)
+        y_mx = [None, None]
 
-        def product(b, q_blocks, copy, staged, bank):
-            acc = psum.tile([P, Q_BLOCKS, P], F32, name="score%d" % bank)
+        def finish(name, v_mx, first_block, q_blocks, copy, acc, queue=nc.sync):
+            width = v_mx[0].shape[1]
             for i, qb in enumerate(q_blocks):
+                cols = slice(qb % 2 * P, (qb % 2 + 1) * P)
                 nc.tensor.matmul_mx(
-                    out=acc[:, i, :], lhsT=y_mx[qb][0][:].bitcast(FP8X4), lhsT_scale=y_mx[qb][1][:],
-                    rhs=v_mx[b][0][:].bitcast(FP8X4), rhs_scale=v_mx[b][1][:], start=True, stop=True,
+                    out=acc[:, i * width : (i + 1) * width],
+                    lhsT=y_mx[qb // 2][0][:, cols].bitcast(FP8X4), lhsT_scale=y_mx[qb // 2][1][:, cols],
+                    rhs=v_mx[0].bitcast(FP8X4), rhs_scale=v_mx[1][:], start=True, stop=True,
                 )
-            copy(staged, acc[:, 0 : len(q_blocks), :])
+            staged = keep.tile([P, len(q_blocks) * width], F32, name=name)
+            copy(staged[:], acc[:, 0 : len(q_blocks) * width])
+            queue.dma_start(
+                out_rows[:, q_blocks[0] : q_blocks[-1] + 1, first_block * P : first_block * P + width],
+                staged[:].rearrange("q (b e) -> q b e", e=width),
+            )
 
         gather_values(0)
-        weigh(0)
-        weigh(1)
-        quantize_v(0)
-        quantize_y(0)
-        weigh(2)
-        quantize_y(1)
-        weigh(3)
-        quantize_y(2)
+        scale_on_vector(0)
+        scale_on_vector(1)
+        scale_on_scalar(2)
+        scale_on_scalar(3)
+        turn_values(0, nc.scalar.copy)
         gather_values(1)
-        quantize_y(3)
-        quantize_v(1)
-        front = keep.tile([P, Q_BLOCKS, 2 * P], F32, name="front")
-        product(0, range(4), nc.scalar.copy, front[:, :, 0:P], 0)
-        product(1, range(4), nc.scalar.copy, front[:, :, P : 2 * P], 1)
-        nc.sync.dma_start(out_rows[:, :, 0 : 2 * P], front[:])
+        y_mx[0] = quantize_y(0, code_tile("y0", 256, "v_pool1")[:])
+        turn_values(1, nc.scalar.copy)
         gather_values(2)
-        quantize_v(2)
-        third = keep.tile([P, Q_BLOCKS, P], F32, name="third")
-        product(2, range(4), nc.scalar.copy, third[:], 2)
-        nc.sync.dma_start(out_rows[:, :, 2 * P : 3 * P], third[:])
+        turn_values(2, nc.scalar.copy)
+        late_codes = code_tile("late", 512, "v_pool2")
+        y_mx[1] = quantize_y(1, late_codes[:, 0:256])
+        v01 = quantize("v01", v_grouped[:, 0:2].rearrange("p b x -> p (b x)"), late_codes[:, 256:512])
         gather_values(3)
-        quantize_v(3)
-        for half, copy in enumerate((nc.scalar.copy, nc.vector.tensor_copy)):
-            last = keep.tile([P, 2, P], F32, name="last%d" % half)
-            product(3, range(2 * half, 2 * half + 2), copy, last[:], 3 * (1 - half))
-            nc.sync.dma_start(out_rows[:, 2 * half : 2 * half + 2, 3 * P : 4 * P], last[:])
+        for h in halves:
+            finish("front%d" % h, v01, 0, (2 * h, 2 * h + 1), nc.scalar.copy, psum.tile([P, 512], F32, name="turn", bufs=2))
+        v2 = quantize("v2", v_grouped[:, 2], code_tile("v2", P, "v_pool3")[:])
+        turn_values(3, nc.vector.tensor_copy)
+        finish("third", v2, 2, (0, 1, 2, 3), nc.scalar.copy, psum.tile([P, 512], F32, name="score2"))
+        v3 = quantize("v3", v_grouped[:, 3], code_tile("v3", P)[:])
+        finish("last0", v3, 3, (0, 1), nc.scalar.copy, psum.tile([P, 512], F32, name="score3"), nc.scalar)
+        finish("last1", v3, 3, (2, 3), nc.vector.tensor_copy, psum.tile([P, 512], F32, name="score0"))

@@ -38,7 +38,7 @@ def tile_attend_at_txl_topk_kernel(tc, uT, pT, k_words, k_scales, c_words, c_sca
         c_byte_pool = keep.tile([P, DISTANCES // 4], I32, name="c_byte_pool")
         k_byte_pool = keep.tile([P, TOKENS // 4], I32, name="k_byte_pool")
         u_raw = keep.tile([P, PACK, QUERIES], F32, name="u_raw")
-        p_raw = [keep.tile([P, PACK, QUERIES // 2], F32, name="p_raw%d" % h) for h in range(2)]
+        p_raw = keep.tile([P, PACK, QUERIES], F32, name="p_raw")
         v_pool = [keep.tile([P, TOKENS], F32, name="v_pool%d" % b, align_bytes=64) for b in range(V_BLOCKS)]
         ls_rows = keep.tile([P, P], F32, name="ls_rows")
         us_cols = keep.tile([P, PACK], F32, name="us_cols")
@@ -58,15 +58,14 @@ def tile_attend_at_txl_topk_kernel(tc, uT, pT, k_words, k_scales, c_words, c_sca
         def words_of(x):
             return x[0].rearrange("p n t -> p (n t)").bitcast(I32)
 
-        nc.sync.dma_start(dist_list[:], offs2)
         nc.sync.dma_start(c_word_pool[:], words_of(c_words))
+        nc.sync.dma_start(dist_list[:], offs2)
         load_scale_rows(c_byte_pool, c_scales, C_PLANE)
         nc.sync.dma_start(k_word_pool[:], words_of(k_words))
         nc.sync.dma_start(tok_list[:], offs)
         load_scale_rows(k_byte_pool, k_scales, 0)
         nc.sync.dma_start(u_raw[:], uT[0].rearrange("(p t) q -> p t q", t=PACK))
-        for h in range(2):
-            nc.sync.dma_start(p_raw[h][:], pT[0].rearrange("(p t) q -> p t q", t=PACK)[:, :, h * 256 : (h + 1) * 256])
+        nc.sync.dma_start(p_raw[:], pT[0].rearrange("(p t) q -> p t q", t=PACK))
         nc.gpsimd.dma_start(ls_rows[0:Q_BLOCKS, :], ls[0].rearrange("o (b m) -> (o b) m", m=P))
         nc.gpsimd.dma_start(us_cols[:], us[0].rearrange("(p t) o -> p (t o)", t=PACK))
         for b in range(V_BLOCKS):
@@ -109,25 +108,25 @@ def tile_attend_at_txl_topk_kernel(tc, uT, pT, k_words, k_scales, c_words, c_sca
                 rhs=codes[:].bitcast(FP8X4), rhs_scale=plane, start=first, stop=not first,
             )
 
-        def content_passes(h, slot):
-            u_mx = quantize("u%d" % h, u_grouped[h][:], code_tile("u%d" % h, 256, slot)[:])
+        def content_passes(h):
+            u_mx = quantize("u%d" % h, u_grouped[h][:], code_tile("u%d" % h, 256)[:])
             for qb in (2 * h, 2 * h + 1):
                 score_pass(qb, u_mx, k_codes, k_bytes[:], True)
 
         def position_passes(h):
-            interleave(nc.scalar.copy, p_grouped[h][:, 0:512], p_raw[h][:, :, 0:P])
-            interleave(nc.vector.tensor_copy, p_grouped[h][:, 512:1024], p_raw[h][:, :, P : 2 * P])
+            interleave(nc.scalar.copy, p_grouped[h][:, 0:512], p_raw[:, :, 2 * h * P : (2 * h + 1) * P])
+            interleave(nc.vector.tensor_copy, p_grouped[h][:, 512:1024], p_raw[:, :, (2 * h + 1) * P : (2 * h + 2) * P])
             p_mx = quantize("p%d" % h, p_grouped[h][:], code_tile("p%d" % h, 256)[:])
             for qb in (2 * h, 2 * h + 1):
                 score_pass(qb, p_mx, c_codes, c_bytes[C_PLANE:P, :], False)
 
         interleave(nc.vector.tensor_copy, u_grouped[0][:], u_raw[:, :, 0:256])
         interleave(nc.scalar.copy, u_grouped[1][:], u_raw[:, :, 256:512])
-        content_passes(0, "")
-        position_passes(0)
-        content_passes(1, "p_grouped0")
-        position_passes(1)
-        weight_tile = keep.tile([P, Q_BLOCKS, PACK, P], F32, name="weights", tag="p_grouped1", align_bytes=64)
+        for h in halves:
+            content_passes(h)
+        for h in halves:
+            position_passes(h)
+        weight_tile = keep.tile([P, Q_BLOCKS, PACK, P], F32, name="weights")
         weights = [weight_tile[:, qb] for qb in range(Q_BLOCKS)]
         for qb in range(Q_BLOCKS):
             nc.scalar.activation(

@@ -139,7 +139,7 @@ def tile_attend_at_txl_topk_kernel(tc, uT, pT, k_words, k_scales, c_words, c_sca
             keep.tile([P, 2, P, PACK], BF16, name="y_grouped%d" % h, tag=("v_pool0", "")[h], align_bytes=64)
             for h in halves
         ]
-        picked = [keep.tile([P, 2, P, 2], BF16, name="picked%d" % b) for b in range(V_BLOCKS)]
+        picked = [keep.tile([P, SLOTS], BF16, name="picked%d" % b) for b in range(V_BLOCKS)]
         v_grouped = keep.tile([P, V_BLOCKS, P * PACK], BF16, name="v_grouped", align_bytes=64)
 
         def turn_weights(qb, turned):
@@ -165,13 +165,13 @@ def tile_attend_at_txl_topk_kernel(tc, uT, pT, k_words, k_scales, c_words, c_sca
             return quantize("y%d" % h, y_grouped[h][:].rearrange("p b q t -> p (b q t)"), codes)
 
         def gather_values(b):
-            nc.vector.tensor_copy(picked[b][:].rearrange("e u p j -> e p u j"), v_pool[b][:].indirect(tok_list[:]))
+            nc.vector.tensor_copy(picked[b][:], v_pool[b][:].indirect(tok_list[:]))
 
         def turn_values(b, copy):
-            pairs = picked[b][:].rearrange("e u p j -> e (u p j)").bitcast(F32)
+            pairs = picked[b][:].bitcast(F32)
             turned = psum.tile([P, PACK, P], F32, name="v_turn", bufs=2)
             for u in range(2):
-                nc.tensor.transpose(turned[:, u, :], pairs[:, u * P : (u + 1) * P], ident[:])
+                nc.tensor.transpose(turned[:, u, :], pairs[:, u : 2 * P : 2], ident[:])
             copy(
                 v_grouped[:, b].bitcast(F32).rearrange("p (e u) -> p e u", u=2),
                 turned[:, 0:2, :].rearrange("p u e -> p e u"),

@@ -21,6 +21,7 @@ VALUES = 512
 Q_BLOCKS = QUERIES // P
 V_BLOCKS = VALUES // P
 C_PLANE = 4
+POOL_BYTES = 4 * TOKENS
 
 FLOPS = 3 * 2 * 512 * 512 * 512
 
@@ -29,6 +30,7 @@ def tile_attend_at_txl_topk_kernel(tc, uT, pT, k_words, k_scales, c_words, c_sca
     nc = tc.nc
     with ExitStack() as ctx:
         keep = ctx.enter_context(tc.tile_pool(name="keep", bufs=1))
+        values = ctx.enter_context(tc.tile_pool(name="values", bufs=1))
         psum = ctx.enter_context(tc.psum_pool(name="psum", bufs=1))
 
         tok_list = keep.tile([P, SLOTS // 16], U16, name="tok_list")
@@ -39,7 +41,13 @@ def tile_attend_at_txl_topk_kernel(tc, uT, pT, k_words, k_scales, c_words, c_sca
         k_byte_pool = keep.tile([P, TOKENS // 4], I32, name="k_byte_pool")
         u_raw = keep.tile([P, PACK, QUERIES], F32, name="u_raw")
         p_raw = keep.tile([P, PACK, QUERIES], F32, name="p_raw")
-        v_pool = [keep.tile([P, TOKENS], F32, name="v_pool%d" % b, align_bytes=64) for b in range(V_BLOCKS)]
+        v_pool = [
+            values.tile([P, TOKENS], F32, name="v_pool%d" % b, align_bytes=64, offset=b * POOL_BYTES) for b in range(V_BLOCKS)
+        ]
+
+        def behind_gather(b, start, shape, dtype, name):
+            return values.tile(shape, dtype, name=name, align_bytes=64, offset=b * POOL_BYTES + start)
+
         ls_rows = keep.tile([P, P], F32, name="ls_rows")
         us_cols = keep.tile([P, PACK], F32, name="us_cols")
         ident = keep.tile([P, P], F32, name="ident")
@@ -135,87 +143,101 @@ def tile_attend_at_txl_topk_kernel(tc, uT, pT, k_words, k_scales, c_words, c_sca
             )
 
         us_wide = us_cols[:].unsqueeze(1).to_broadcast([P, P, PACK])
-        y_grouped = [
-            keep.tile([P, 2, P, PACK], BF16, name="y_grouped%d" % h, tag=("v_pool0", "")[h], align_bytes=64)
-            for h in halves
-        ]
         picked = [keep.tile([P, SLOTS], BF16, name="picked%d" % b) for b in range(V_BLOCKS)]
-        v_grouped = keep.tile([P, V_BLOCKS, P * PACK], BF16, name="v_grouped", align_bytes=64)
 
-        def turn_weights(qb, turned):
+        def scale_on_vector(qb, b):
+            turned = psum.tile([P, PACK, P], F32, name="turn", bufs=2)
             for t in range(PACK):
                 nc.tensor.transpose(turned[:, t, :], weights[qb][:, t, :], ident[:])
-            return turned
+            grouped = behind_gather(b, qb * 1024, [P, P, PACK], BF16, "y_grouped%d" % qb)
+            nc.vector.tensor_tensor(grouped[:], turned[:].rearrange("p t q -> p q t"), us_wide, mybir.AluOpType.mult)
+            return grouped[:].rearrange("p q t -> p (q t)")
 
-        def scale_on_vector(qb):
-            turned = turn_weights(qb, psum.tile([P, PACK, P], F32, name="turn", bufs=2))
-            nc.vector.tensor_tensor(
-                y_grouped[0][:, qb], turned[:].rearrange("p t q -> p q t"), us_wide, mybir.AluOpType.mult
+        def scale_on_scalar(q_blocks):
+            y_pairs = keep.tile([P, 2, 2 * P, 2], BF16, name="y_pairs", align_bytes=64)
+            for i, qb in enumerate(q_blocks):
+                turned = psum.tile([P, PACK, P], F32, name="score%d" % i)
+                for t in range(PACK):
+                    nc.tensor.transpose(turned[:, t, :], weights[qb][:, t, :], ident[:])
+                for t in range(PACK):
+                    nc.scalar.activation(
+                        y_pairs[:, t // 2, i * P : (i + 1) * P, t % 2], turned[:, t, :],
+                        mybir.ActivationFunctionType.Copy, scale=us_cols[:, t : t + 1],
+                    )
+            grouped = keep.tile([P, 2 * P * PACK], BF16, name="y_grouped_mid", align_bytes=64)
+            nc.scalar.copy(
+                grouped[:].bitcast(F32).rearrange("p (q u) -> p q u", u=2),
+                y_pairs[:].rearrange("p u q j -> p (u q j)").bitcast(F32).rearrange("p (u q) -> p q u", u=2),
             )
-
-        def scale_on_scalar(qb):
-            turned = turn_weights(qb, psum.tile([P, PACK, P], F32, name="score%d" % (qb - 2)))
-            for t in range(PACK):
-                nc.scalar.activation(
-                    y_grouped[1][:, qb - 2, :, t], turned[:, t, :],
-                    mybir.ActivationFunctionType.Copy, scale=us_cols[:, t : t + 1],
-                )
-
-        def quantize_y(h, codes):
-            return quantize("y%d" % h, y_grouped[h][:].rearrange("p b q t -> p (b q t)"), codes)
+            return grouped[:]
 
         def gather_values(b):
             nc.vector.tensor_copy(picked[b][:], v_pool[b][:].indirect(tok_list[:]))
 
-        def turn_values(b, copy):
+        def turn_values(b):
             pairs = picked[b][:].bitcast(F32)
             turned = psum.tile([P, PACK, P], F32, name="v_turn", bufs=2)
             for u in range(2):
                 nc.tensor.transpose(turned[:, u, :], pairs[:, u : 2 * P : 2], ident[:])
-            copy(
-                v_grouped[:, b].bitcast(F32).rearrange("p (e u) -> p e u", u=2),
+            nc.scalar.copy(
+                v_grouped[b].bitcast(F32).rearrange("p (e u) -> p e u", u=2),
                 turned[:, 0:2, :].rearrange("p u e -> p e u"),
             )
 
         out_rows = out[0].rearrange("(b q) e -> q b e", q=P)
-        y_mx = [None, None]
 
-        def finish(name, v_mx, first_block, q_blocks, copy, acc, queue=nc.sync):
+        def product(acc, qb, v_mx):
+            nc.tensor.matmul_mx(
+                out=acc, lhsT=y_mx[qb][0].bitcast(FP8X4), lhsT_scale=y_mx[qb][1],
+                rhs=v_mx[0].bitcast(FP8X4), rhs_scale=v_mx[1][:], start=True, stop=True,
+            )
+
+        def finish(v_mx, first_block, q_blocks, copy, acc, staged):
             width = v_mx[0].shape[1]
             for i, qb in enumerate(q_blocks):
-                cols = slice(qb % 2 * P, (qb % 2 + 1) * P)
-                nc.tensor.matmul_mx(
-                    out=acc[:, i * width : (i + 1) * width],
-                    lhsT=y_mx[qb // 2][0][:, cols].bitcast(FP8X4), lhsT_scale=y_mx[qb // 2][1][:, cols],
-                    rhs=v_mx[0].bitcast(FP8X4), rhs_scale=v_mx[1][:], start=True, stop=True,
-                )
-            staged = keep.tile([P, len(q_blocks) * width], F32, name=name)
+                product(acc[:, i * width : (i + 1) * width], qb, v_mx)
             copy(staged[:], acc[:, 0 : len(q_blocks) * width])
-            queue.dma_start(
+            nc.sync.dma_start(
                 out_rows[:, q_blocks[0] : q_blocks[-1] + 1, first_block * P : first_block * P + width],
                 staged[:].rearrange("q (b e) -> q b e", e=width),
             )
 
         gather_values(0)
-        scale_on_vector(0)
-        scale_on_vector(1)
-        scale_on_scalar(2)
-        scale_on_scalar(3)
-        turn_values(0, nc.scalar.copy)
+        y_early = [scale_on_vector(qb, 0) for qb in range(2)]
+        y_mx = [quantize("y%d" % qb, y_early[qb], code_tile("y%d" % qb, P)[:]) for qb in range(2)]
+        y_mx = [(codes, scales[:]) for codes, scales in y_mx]
+        y_late = scale_on_scalar((2, 3))
+        v_front = keep.tile([P, 2, P * PACK], BF16, name="v_front", tag="y_pairs", align_bytes=64)
+        v_back = keep.tile([P, 2, P * PACK], BF16, name="v_back", align_bytes=64)
+        v_grouped = [v_front[:, 0], v_front[:, 1], v_back[:, 0], v_back[:, 1]]
+        turn_values(0)
         gather_values(1)
-        y_mx[0] = quantize_y(0, code_tile("y0", 256, "v_pool1")[:])
-        turn_values(1, nc.scalar.copy)
+        turn_values(1)
         gather_values(2)
-        turn_values(2, nc.scalar.copy)
-        late_codes = code_tile("late", 512, "v_pool2")
-        y_mx[1] = quantize_y(1, late_codes[:, 0:256])
-        v01 = quantize("v01", v_grouped[:, 0:2].rearrange("p b x -> p (b x)"), late_codes[:, 256:512])
-        gather_values(3)
+        turn_values(2)
+        after_2 = behind_gather(2, 0, [P, 4 * P], U32, "after_2")
+        y23 = quantize("y23", y_late, after_2[:, 0 : 2 * P])
+        v01 = quantize("v01", v_front[:].rearrange("p b x -> p (b x)"), after_2[:, 2 * P : 4 * P])
+        y_mx.extend((y23[0][:, i * P : (i + 1) * P], y23[1][:, i * P : (i + 1) * P]) for i in range(2))
         for h in halves:
-            finish("front%d" % h, v01, 0, (2 * h, 2 * h + 1), nc.scalar.copy, psum.tile([P, 512], F32, name="turn", bufs=2))
-        v2 = quantize("v2", v_grouped[:, 2], code_tile("v2", P, "v_pool3")[:])
-        turn_values(3, nc.vector.tensor_copy)
-        finish("third", v2, 2, (0, 1, 2, 3), nc.scalar.copy, psum.tile([P, 512], F32, name="score2"))
-        v3 = quantize("v3", v_grouped[:, 3], code_tile("v3", P)[:])
-        finish("last0", v3, 3, (0, 1), nc.scalar.copy, psum.tile([P, 512], F32, name="score3"), nc.scalar)
-        finish("last1", v3, 3, (2, 3), nc.vector.tensor_copy, psum.tile([P, 512], F32, name="score0"))
+            finish(
+                v01, 0, (2 * h, 2 * h + 1), nc.scalar.copy, psum.tile([P, 512], F32, name="turn", bufs=2),
+                keep.tile([P, 512], F32, name="front%d" % h),
+            )
+        gather_values(3)
+        turn_values(3)
+        v2 = quantize("v2", v_grouped[2], behind_gather(3, 0, [P, P], U32, "v2_codes")[:])
+        for h in halves:
+            finish(
+                v2, 2, (2 * h, 2 * h + 1), (nc.scalar.copy, nc.vector.tensor_copy)[h],
+                psum.tile([P, 512], F32, name=("score2", "v_turn")[h], bufs=(1, 2)[h]),
+                keep.tile([P, 256], F32, name="third%d" % h),
+            )
+        v3 = quantize("v3", v_grouped[3], code_tile("v3", P)[:])
+        last_staged = [keep.tile([P, 2, P], F32, name="last%d" % e) for e in range(2)]
+        for qb in range(Q_BLOCKS):
+            acc = psum.tile([P, 512], F32, name=("score3", "score0", "score1", "turn")[qb], bufs=(1, 1, 1, 2)[qb])
+            product(acc[:, 0:P], qb, v3)
+            (nc.vector.tensor_copy, nc.scalar.copy)[qb % 2](last_staged[qb % 2][:, qb // 2, :], acc[:, 0:P])
+        nc.sync.dma_start(out_rows[:, 0:4:2, 3 * P : 4 * P], last_staged[0][:])
+        nc.scalar.dma_start(out_rows[:, 1:4:2, 3 * P : 4 * P], last_staged[1][:])

@@ -227,13 +227,13 @@ def tile_attend_at_txl_topk_kernel(tc, uT, pT, k_words, k_scales, c_words, c_sca
         gather_values(3)
         turn_values(3)
         v2 = quantize("v2", v_grouped[2], behind_gather(3, 0, [P, P], U32, "v2_codes")[:])
+        v3 = quantize("v3", v_grouped[3], code_tile("v3", P)[:])
         for h in halves:
             finish(
                 v2, 2, (2 * h, 2 * h + 1), (nc.scalar.copy, nc.vector.tensor_copy)[h],
                 psum.tile([P, 512], F32, name=("score2", "v_turn")[h], bufs=(1, 2)[h]),
-                keep.tile([P, 256], F32, name="third%d" % h),
+                keep.tile([P, 256], F32, name="third%d" % h, tag=("", "v_back")[h], align_bytes=64),
             )
-        v3 = quantize("v3", v_grouped[3], code_tile("v3", P)[:])
         last_staged = [keep.tile([P, 2, P], F32, name="last%d" % e) for e in range(2)]
         for qb in range(Q_BLOCKS):
             acc = psum.tile([P, 512], F32, name=("score3", "score0", "score1", "turn")[qb], bufs=(1, 1, 1, 2)[qb])

@@ -36,9 +36,11 @@ def tile_attend_at_txl_topk_kernel(tc, uT, pT, k_words, k_scales, c_words, c_sca
         tok_list = keep.tile([P, SLOTS // 16], U16, name="tok_list")
         dist_list = keep.tile([P, SLOTS // 16], U16, name="dist_list")
         c_word_pool = keep.tile([P, DISTANCES], I32, name="c_word_pool")
-        k_word_pool = keep.tile([P, TOKENS], I32, name="k_word_pool")
-        c_byte_pool = keep.tile([P, DISTANCES // 4], I32, name="c_byte_pool")
-        k_byte_pool = keep.tile([P, TOKENS // 4], I32, name="k_byte_pool")
+        k_word_pool = values.tile([P, TOKENS], I32, name="k_word_pool", align_bytes=64, offset=(V_BLOCKS + 2) * POOL_BYTES)
+        c_byte_pool = values.tile(
+            [P, DISTANCES // 4], I32, name="c_byte_pool", align_bytes=64, offset=(V_BLOCKS + 1) * POOL_BYTES
+        )
+        k_byte_pool = values.tile([P, TOKENS // 4], I32, name="k_byte_pool", align_bytes=64, offset=V_BLOCKS * POOL_BYTES)
         u_raw = keep.tile([P, PACK, QUERIES], F32, name="u_raw")
         p_raw = keep.tile([P, PACK, QUERIES], F32, name="p_raw")
         v_pool = [
@@ -51,7 +53,6 @@ def tile_attend_at_txl_topk_kernel(tc, uT, pT, k_words, k_scales, c_words, c_sca
         ls_rows = keep.tile([P, P], F32, name="ls_rows")
         us_cols = keep.tile([P, PACK], F32, name="us_cols")
         ident = keep.tile([P, P], F32, name="ident")
-        neg_ls = keep.tile([P, Q_BLOCKS], F32, name="neg_ls")
 
         nc.gpsimd.memset(c_byte_pool[:], 0)
         nc.gpsimd.memset(k_byte_pool[:], 0)
@@ -68,12 +69,12 @@ def tile_attend_at_txl_topk_kernel(tc, uT, pT, k_words, k_scales, c_words, c_sca
 
         nc.sync.dma_start(c_word_pool[:], words_of(c_words))
         nc.sync.dma_start(dist_list[:], offs2)
+        nc.sync.dma_start(p_raw[:], pT[0].rearrange("(p t) q -> p t q", t=PACK))
         load_scale_rows(c_byte_pool, c_scales, C_PLANE)
-        nc.sync.dma_start(k_word_pool[:], words_of(k_words))
+        nc.sync.dma_start(u_raw[:], uT[0].rearrange("(p t) q -> p t q", t=PACK))
         nc.sync.dma_start(tok_list[:], offs)
         load_scale_rows(k_byte_pool, k_scales, 0)
-        nc.sync.dma_start(u_raw[:], uT[0].rearrange("(p t) q -> p t q", t=PACK))
-        nc.sync.dma_start(p_raw[:], pT[0].rearrange("(p t) q -> p t q", t=PACK))
+        nc.sync.dma_start(k_word_pool[:], words_of(k_words))
         nc.gpsimd.dma_start(ls_rows[0:Q_BLOCKS, :], ls[0].rearrange("o (b m) -> (o b) m", m=P))
         nc.gpsimd.dma_start(us_cols[:], us[0].rearrange("(p t) o -> p (t o)", t=PACK))
         for b in range(V_BLOCKS):
@@ -85,7 +86,6 @@ def tile_attend_at_txl_topk_kernel(tc, uT, pT, k_words, k_scales, c_words, c_sca
         k_bytes = keep.tile([P, SLOTS], U8, name="k_bytes", align_bytes=64)
         nc.vector.tensor_copy(c_codes[:], c_word_pool[:].bitcast(U32).indirect(dist_list[:]))
         nc.vector.tensor_copy(c_bytes[:], c_byte_pool[:].bitcast(U8).indirect(dist_list[:]))
-        nc.vector.tensor_copy(k_codes[:], k_word_pool[:].bitcast(U32).indirect(tok_list[:]))
         nc.vector.tensor_copy(k_bytes[:], k_byte_pool[:].bitcast(U8).indirect(tok_list[:]))
 
         def interleave(copy, grouped, raw):
@@ -102,7 +102,6 @@ def tile_attend_at_txl_topk_kernel(tc, uT, pT, k_words, k_scales, c_words, c_sca
 
         ls_turn = psum.tile([P, PACK, P], F32, name="turn", bufs=2)
         nc.tensor.transpose(ls_turn[:, 0, :], ls_rows[:], ident[:])
-        nc.scalar.mul(neg_ls[:], ls_turn[:, 0, 0:Q_BLOCKS], -1.0)
 
         halves = range(2)
         u_grouped = [keep.tile([P, 2 * P * PACK], BF16, name="u_grouped%d" % h, align_bytes=64) for h in halves]
@@ -116,24 +115,22 @@ def tile_attend_at_txl_topk_kernel(tc, uT, pT, k_words, k_scales, c_words, c_sca
                 rhs=codes[:].bitcast(FP8X4), rhs_scale=plane, start=first, stop=not first,
             )
 
-        def content_passes(h):
-            u_mx = quantize("u%d" % h, u_grouped[h][:], code_tile("u%d" % h, 256)[:])
-            for qb in (2 * h, 2 * h + 1):
-                score_pass(qb, u_mx, k_codes, k_bytes[:], True)
-
-        def position_passes(h):
-            interleave(nc.scalar.copy, p_grouped[h][:, 0:512], p_raw[:, :, 2 * h * P : (2 * h + 1) * P])
-            interleave(nc.vector.tensor_copy, p_grouped[h][:, 512:1024], p_raw[:, :, (2 * h + 1) * P : (2 * h + 2) * P])
-            p_mx = quantize("p%d" % h, p_grouped[h][:], code_tile("p%d" % h, 256)[:])
-            for qb in (2 * h, 2 * h + 1):
-                score_pass(qb, p_mx, c_codes, c_bytes[C_PLANE:P, :], False)
-
-        interleave(nc.vector.tensor_copy, u_grouped[0][:], u_raw[:, :, 0:256])
-        interleave(nc.scalar.copy, u_grouped[1][:], u_raw[:, :, 256:512])
         for h in halves:
-            content_passes(h)
+            interleave(nc.scalar.copy, p_grouped[h][:], p_raw[:, :, 256 * h : 256 * (h + 1)])
+        p_codes = [behind_gather(V_BLOCKS + 1, 0, [P, 256], U32, "p0_codes"), code_tile("p1", 256)]
         for h in halves:
-            position_passes(h)
+            p_mx = quantize("p%d" % h, p_grouped[h][:], p_codes[h][:])
+            for qb in (2 * h, 2 * h + 1):
+                score_pass(qb, p_mx, c_codes, c_bytes[C_PLANE:P, :], True)
+        for h in halves:
+            interleave(nc.scalar.copy, u_grouped[h][:], u_raw[:, :, 256 * h : 256 * (h + 1)])
+        neg_ls = keep.tile([P, Q_BLOCKS], F32, name="neg_ls", tag="u_raw")
+        nc.scalar.mul(neg_ls[:], ls_turn[:, 0, 0:Q_BLOCKS], -1.0)
+        nc.vector.tensor_copy(k_codes[:], k_word_pool[:].bitcast(U32).indirect(tok_list[:]))
+        for h in halves:
+            u_mx = quantize("u%d" % h, u_grouped[h][:], behind_gather(V_BLOCKS + 2 * h, 0, [P, 256], U32, "u%d_codes" % h)[:])
+            for qb in (2 * h, 2 * h + 1):
+                score_pass(qb, u_mx, k_codes, k_bytes[:], False)
         weight_tile = keep.tile([P, Q_BLOCKS, PACK, P], F32, name="weights")
         weights = [weight_tile[:, qb] for qb in range(Q_BLOCKS)]
         for qb in range(Q_BLOCKS):
@@ -145,13 +142,11 @@ def tile_attend_at_txl_topk_kernel(tc, uT, pT, k_words, k_scales, c_words, c_sca
         us_wide = us_cols[:].unsqueeze(1).to_broadcast([P, P, PACK])
         picked = [keep.tile([P, SLOTS], BF16, name="picked%d" % b) for b in range(V_BLOCKS)]
 
-        def scale_on_vector(qb, b):
+        def scale_on_vector(qb, grouped):
             turned = psum.tile([P, PACK, P], F32, name="turn", bufs=2)
             for t in range(PACK):
                 nc.tensor.transpose(turned[:, t, :], weights[qb][:, t, :], ident[:])
-            grouped = behind_gather(b, qb * 1024, [P, P, PACK], BF16, "y_grouped%d" % qb)
-            nc.vector.tensor_tensor(grouped[:], turned[:].rearrange("p t q -> p q t"), us_wide, mybir.AluOpType.mult)
-            return grouped[:].rearrange("p q t -> p (q t)")
+            nc.vector.tensor_tensor(grouped, turned[:].rearrange("p t q -> p q t"), us_wide, mybir.AluOpType.mult)
 
         def scale_on_scalar(q_blocks):
             y_pairs = keep.tile([P, 2, 2 * P, 2], BF16, name="y_pairs", align_bytes=64)
@@ -202,23 +197,25 @@ def tile_attend_at_txl_topk_kernel(tc, uT, pT, k_words, k_scales, c_words, c_sca
                 staged[:].rearrange("q (b e) -> q b e", e=width),
             )
 
-        gather_values(0)
-        y_early = [scale_on_vector(qb, 0) for qb in range(2)]
-        y_mx = [quantize("y%d" % qb, y_early[qb], code_tile("y%d" % qb, P)[:]) for qb in range(2)]
-        y_mx = [(codes, scales[:]) for codes, scales in y_mx]
-        y_late = scale_on_scalar((2, 3))
-        v_front = keep.tile([P, 2, P * PACK], BF16, name="v_front", tag="y_pairs", align_bytes=64)
+        v_front = keep.tile([P, 2, P * PACK], BF16, name="v_front", align_bytes=64)
         v_back = keep.tile([P, 2, P * PACK], BF16, name="v_back", align_bytes=64)
         v_grouped = [v_front[:, 0], v_front[:, 1], v_back[:, 0], v_back[:, 1]]
+        gather_values(0)
+        y_early = behind_gather(0, 0, [P, 2 * P, PACK], BF16, "y_early")
+        for qb in range(2):
+            scale_on_vector(qb, y_early[:, qb * P : (qb + 1) * P, :])
         turn_values(0)
+        y_late = scale_on_scalar((2, 3))
         gather_values(1)
         turn_values(1)
+        y01 = quantize("y01", y_early[:].rearrange("p q t -> p (q t)"), behind_gather(1, 0, [P, 2 * P], U32, "y01_codes")[:])
         gather_values(2)
         turn_values(2)
-        after_2 = behind_gather(2, 0, [P, 4 * P], U32, "after_2")
-        y23 = quantize("y23", y_late, after_2[:, 0 : 2 * P])
-        v01 = quantize("v01", v_front[:].rearrange("p b x -> p (b x)"), after_2[:, 2 * P : 4 * P])
-        y_mx.extend((y23[0][:, i * P : (i + 1) * P], y23[1][:, i * P : (i + 1) * P]) for i in range(2))
+        v01 = quantize(
+            "v01", v_front[:].rearrange("p b x -> p (b x)"), behind_gather(2, 0, [P, 2 * P], U32, "v01_codes")[:]
+        )
+        y23 = quantize("y23", y_late, behind_gather(2, 1024, [P, 2 * P], U32, "y23_codes")[:])
+        y_mx = [(y[0][:, i * P : (i + 1) * P], y[1][:, i * P : (i + 1) * P]) for y in (y01, y23) for i in range(2)]
         for h in halves:
             finish(
                 v01, 0, (2 * h, 2 * h + 1), nc.scalar.copy, psum.tile([P, 512], F32, name="turn", bufs=2),

@@ -59,21 +59,26 @@ def tile_attend_at_txl_topk_kernel(tc, uT, pT, k_words, k_scales, c_words, c_sca
         nc.gpsimd.memset(ls_rows[:], 0.0)
         make_identity(nc, ident[:])
 
-        def load_scale_rows(pool_tile, rows, first):
-            rows = rows[0].bitcast(I32)
-            for r in range(4):
-                nc.sync.dma_start(pool_tile[first + r : P : 32, :], rows[r:16:4, :])
+        def load_scale_rows(pool_tile, rows, first, r):
+            nc.sync.dma_start(pool_tile[first + r : P : 32, :], rows[0].bitcast(I32)[r:16:4, :])
 
         def words_of(x):
             return x[0].rearrange("p n t -> p (n t)").bitcast(I32)
 
         nc.sync.dma_start(c_word_pool[:], words_of(c_words))
         nc.sync.dma_start(dist_list[:], offs2)
-        nc.sync.dma_start(p_raw[:], pT[0].rearrange("(p t) q -> p t q", t=PACK))
-        load_scale_rows(c_byte_pool, c_scales, C_PLANE)
-        nc.sync.dma_start(u_raw[:], uT[0].rearrange("(p t) q -> p t q", t=PACK))
+        scale_loads = [
+            (pool_tile, rows, first, r)
+            for r in range(4)
+            for pool_tile, rows, first in ((c_byte_pool, c_scales, C_PLANE), (k_byte_pool, k_scales, 0))
+        ]
         nc.sync.dma_start(tok_list[:], offs)
-        load_scale_rows(k_byte_pool, k_scales, 0)
+        for load in scale_loads[:4]:
+            load_scale_rows(*load)
+        nc.sync.dma_start(p_raw[:], pT[0].rearrange("(p t) q -> p t q", t=PACK))
+        for load in scale_loads[4:]:
+            load_scale_rows(*load)
+        nc.sync.dma_start(u_raw[:], uT[0].rearrange("(p t) q -> p t q", t=PACK))
         nc.sync.dma_start(k_word_pool[:], words_of(k_words))
         nc.gpsimd.dma_start(ls_rows[0:Q_BLOCKS, :], ls[0].rearrange("o (b m) -> (o b) m", m=P))
         nc.gpsimd.dma_start(us_cols[:], us[0].rearrange("(p t) o -> p (t o)", t=PACK))
@@ -117,20 +122,22 @@ def tile_attend_at_txl_topk_kernel(tc, uT, pT, k_words, k_scales, c_words, c_sca
 
         for h in halves:
             interleave(nc.scalar.copy, p_grouped[h][:], p_raw[:, :, 256 * h : 256 * (h + 1)])
-        p_codes = [behind_gather(V_BLOCKS + 1, 0, [P, 256], U32, "p0_codes"), code_tile("p1", 256)]
-        for h in halves:
-            p_mx = quantize("p%d" % h, p_grouped[h][:], p_codes[h][:])
+
+        def passes(name, h, grouped, codes, table_codes, plane, first):
+            mx = quantize("%s%d" % (name, h), grouped[h][:], codes[:])
             for qb in (2 * h, 2 * h + 1):
-                score_pass(qb, p_mx, c_codes, c_bytes[C_PLANE:P, :], True)
+                score_pass(qb, mx, table_codes, plane, first)
+
+        for h in halves:
+            codes = behind_gather(V_BLOCKS + 1 - h, 0, [P, 256], U32, "p%d_codes" % h)
+            passes("p", h, p_grouped, codes, c_codes, c_bytes[C_PLANE:P, :], True)
         for h in halves:
             interleave(nc.scalar.copy, u_grouped[h][:], u_raw[:, :, 256 * h : 256 * (h + 1)])
         neg_ls = keep.tile([P, Q_BLOCKS], F32, name="neg_ls", tag="u_raw")
         nc.scalar.mul(neg_ls[:], ls_turn[:, 0, 0:Q_BLOCKS], -1.0)
         nc.vector.tensor_copy(k_codes[:], k_word_pool[:].bitcast(U32).indirect(tok_list[:]))
-        for h in halves:
-            u_mx = quantize("u%d" % h, u_grouped[h][:], behind_gather(V_BLOCKS + 2 * h, 0, [P, 256], U32, "u%d_codes" % h)[:])
-            for qb in (2 * h, 2 * h + 1):
-                score_pass(qb, u_mx, k_codes, k_bytes[:], False)
+        passes("u", 0, u_grouped, code_tile("u0", 256), k_codes, k_bytes[:], False)
+        passes("u", 1, u_grouped, behind_gather(V_BLOCKS + 2, 0, [P, 256], U32, "u1_codes"), k_codes, k_bytes[:], False)
         weight_tile = keep.tile([P, Q_BLOCKS, PACK, P], F32, name="weights")
         weights = [weight_tile[:, qb] for qb in range(Q_BLOCKS)]
         for qb in range(Q_BLOCKS):
@@ -211,10 +218,10 @@ def tile_attend_at_txl_topk_kernel(tc, uT, pT, k_words, k_scales, c_words, c_sca
         y01 = quantize("y01", y_early[:].rearrange("p q t -> p (q t)"), behind_gather(1, 0, [P, 2 * P], U32, "y01_codes")[:])
         gather_values(2)
         turn_values(2)
+        y23 = quantize("y23", y_late, behind_gather(2, 1024, [P, 2 * P], U32, "y23_codes")[:])
         v01 = quantize(
             "v01", v_front[:].rearrange("p b x -> p (b x)"), behind_gather(2, 0, [P, 2 * P], U32, "v01_codes")[:]
         )
-        y23 = quantize("y23", y_late, behind_gather(2, 1024, [P, 2 * P], U32, "y23_codes")[:])
         y_mx = [(y[0][:, i * P : (i + 1) * P], y[1][:, i * P : (i + 1) * P]) for y in (y01, y23) for i in range(2)]
         for h in halves:
             finish(
@@ -235,6 +242,6 @@ def tile_attend_at_txl_topk_kernel(tc, uT, pT, k_words, k_scales, c_words, c_sca
         for qb in range(Q_BLOCKS):
             acc = psum.tile([P, 512], F32, name=("score3", "score0", "score1", "turn")[qb], bufs=(1, 1, 1, 2)[qb])
             product(acc[:, 0:P], qb, v3)
-            (nc.vector.tensor_copy, nc.scalar.copy)[qb % 2](last_staged[qb % 2][:, qb // 2, :], acc[:, 0:P])
-        nc.sync.dma_start(out_rows[:, 0:4:2, 3 * P : 4 * P], last_staged[0][:])
-        nc.scalar.dma_start(out_rows[:, 1:4:2, 3 * P : 4 * P], last_staged[1][:])
+            (nc.vector.tensor_copy, nc.scalar.copy)[qb // 2](last_staged[qb // 2][:, qb % 2, :], acc[:, 0:P])
+        nc.sync.dma_start(out_rows[:, 0:2, 3 * P : 4 * P], last_staged[0][:])
+        nc.scalar.dma_start(out_rows[:, 2:4, 3 * P : 4 * P], last_staged[1][:])

@@ -67,17 +67,17 @@ def tile_attend_at_txl_topk_kernel(tc, uT, pT, k_words, k_scales, c_words, c_sca
 
         nc.sync.dma_start(c_word_pool[:], words_of(c_words))
         nc.sync.dma_start(dist_list[:], offs2)
-        scale_loads = [
-            (pool_tile, rows, first, r)
-            for r in range(4)
-            for pool_tile, rows, first in ((c_byte_pool, c_scales, C_PLANE), (k_byte_pool, k_scales, 0))
-        ]
         nc.sync.dma_start(tok_list[:], offs)
-        for load in scale_loads[:4]:
-            load_scale_rows(*load)
+
+        def load_scale_rows_of_both(rows_in_quadrant):
+            for r in rows_in_quadrant:
+                load_scale_rows(c_byte_pool, c_scales, C_PLANE, r)
+            for r in rows_in_quadrant:
+                load_scale_rows(k_byte_pool, k_scales, 0, r)
+
+        load_scale_rows_of_both((0, 1))
         nc.sync.dma_start(p_raw[:], pT[0].rearrange("(p t) q -> p t q", t=PACK))
-        for load in scale_loads[4:]:
-            load_scale_rows(*load)
+        load_scale_rows_of_both((2, 3))
         nc.sync.dma_start(u_raw[:], uT[0].rearrange("(p t) q -> p t q", t=PACK))
         nc.sync.dma_start(k_word_pool[:], words_of(k_words))
         nc.gpsimd.dma_start(ls_rows[0:Q_BLOCKS, :], ls[0].rearrange("o (b m) -> (o b) m", m=P))
@@ -234,9 +234,9 @@ def tile_attend_at_txl_topk_kernel(tc, uT, pT, k_words, k_scales, c_words, c_sca
         v3 = quantize("v3", v_grouped[3], code_tile("v3", P)[:])
         for h in halves:
             finish(
-                v2, 2, (2 * h, 2 * h + 1), (nc.scalar.copy, nc.vector.tensor_copy)[h],
+                v2, 2, (2 * h, 2 * h + 1), nc.scalar.copy,
                 psum.tile([P, 512], F32, name=("score2", "v_turn")[h], bufs=(1, 2)[h]),
-                keep.tile([P, 256], F32, name="third%d" % h, tag=("", "v_back")[h], align_bytes=64),
+                keep.tile([P, 256], F32, name="third%d" % h),
             )
         last_staged = [keep.tile([P, 2, P], F32, name="last%d" % e) for e in range(2)]
         for qb in range(Q_BLOCKS):

@@ -194,10 +194,12 @@ def tile_attend_at_txl_topk_kernel(tc, uT, pT, k_words, k_scales, c_words, c_sca
                 rhs=v_mx[0].bitcast(FP8X4), rhs_scale=v_mx[1][:], start=True, stop=True,
             )
 
-        def finish(v_mx, first_block, q_blocks, copy, acc, staged):
+        def products(v_mx, q_blocks, acc):
             width = v_mx[0].shape[1]
             for i, qb in enumerate(q_blocks):
                 product(acc[:, i * width : (i + 1) * width], qb, v_mx)
+
+        def empty(acc, first_block, width, q_blocks, copy, staged):
             copy(staged[:], acc[:, 0 : len(q_blocks) * width])
             nc.sync.dma_start(
                 out_rows[:, q_blocks[0] : q_blocks[-1] + 1, first_block * P : first_block * P + width],
@@ -223,21 +225,24 @@ def tile_attend_at_txl_topk_kernel(tc, uT, pT, k_words, k_scales, c_words, c_sca
             "v01", v_front[:].rearrange("p b x -> p (b x)"), behind_gather(2, 0, [P, 2 * P], U32, "v01_codes")[:]
         )
         y_mx = [(y[0][:, i * P : (i + 1) * P], y[1][:, i * P : (i + 1) * P]) for y in (y01, y23) for i in range(2)]
-        for h in halves:
-            finish(
-                v01, 0, (2 * h, 2 * h + 1), nc.scalar.copy, psum.tile([P, 512], F32, name="turn", bufs=2),
-                keep.tile([P, 512], F32, name="front%d" % h),
-            )
+        acc = psum.tile([P, 512], F32, name="turn", bufs=2)
+        products(v01, (0, 1), acc)
+        empty(acc, 0, 2 * P, (0, 1), nc.scalar.copy, keep.tile([P, 512], F32, name="front0"))
+        front_banks = [psum.tile([P, 512], F32, name="turn", bufs=2), psum.tile([P, 512], F32, name="score3")]
+        for i in range(2):
+            products(v01, (2 + i,), front_banks[i])
         gather_values(3)
+        front_late = behind_gather(3, 1024, [P, 2, 2 * P], F32, "front_late")
+        nc.scalar.copy(front_late[:, 0], front_banks[0][:, 0 : 2 * P])
         turn_values(3)
         v2 = quantize("v2", v_grouped[2], behind_gather(3, 0, [P, P], U32, "v2_codes")[:])
+        nc.vector.tensor_copy(front_late[:, 1], front_banks[1][:, 0 : 2 * P])
+        nc.sync.dma_start(out_rows[:, 2:4, 0 : 2 * P], front_late[:])
         v3 = quantize("v3", v_grouped[3], code_tile("v3", P)[:])
         for h in halves:
-            finish(
-                v2, 2, (2 * h, 2 * h + 1), nc.scalar.copy,
-                psum.tile([P, 512], F32, name=("score2", "v_turn")[h], bufs=(1, 2)[h]),
-                keep.tile([P, 256], F32, name="third%d" % h),
-            )
+            acc = psum.tile([P, 512], F32, name=("score2", "v_turn")[h], bufs=(1, 2)[h])
+            products(v2, (2 * h, 2 * h + 1), acc)
+            empty(acc, 2, P, (2 * h, 2 * h + 1), nc.scalar.copy, keep.tile([P, 256], F32, name="third%d" % h))
         last_staged = [keep.tile([P, 2, P], F32, name="last%d" % e) for e in range(2)]
         for qb in range(Q_BLOCKS):
             acc = psum.tile([P, 512], F32, name=("score3", "score0", "score1", "turn")[qb], bufs=(1, 1, 1, 2)[qb])

@@ -78,10 +78,10 @@ def tile_attend_at_txl_topk_kernel(tc, uT, pT, k_words, k_scales, c_words, c_sca
         load_scale_rows_of_both((0, 1))
         nc.sync.dma_start(p_raw[:], pT[0].rearrange("(p t) q -> p t q", t=PACK))
         load_scale_rows_of_both((2, 3))
+        nc.sync.dma_start(us_cols[:], us[0].rearrange("(p t) o -> p (t o)", t=PACK))
         nc.sync.dma_start(u_raw[:], uT[0].rearrange("(p t) q -> p t q", t=PACK))
         nc.sync.dma_start(k_word_pool[:], words_of(k_words))
         nc.gpsimd.dma_start(ls_rows[0:Q_BLOCKS, :], ls[0].rearrange("o (b m) -> (o b) m", m=P))
-        nc.gpsimd.dma_start(us_cols[:], us[0].rearrange("(p t) o -> p (t o)", t=PACK))
         for b in range(V_BLOCKS):
             nc.sync.dma_start(v_pool[b][:], vT[b * P : (b + 1) * P, :])
 
@@ -107,6 +107,12 @@ def tile_attend_at_txl_topk_kernel(tc, uT, pT, k_words, k_scales, c_words, c_sca
 
         ls_turn = psum.tile([P, PACK, P], F32, name="turn", bufs=2)
         nc.tensor.transpose(ls_turn[:, 0, :], ls_rows[:], ident[:])
+
+        us_turn = psum.tile([P, PACK, P], F32, name="turn", bufs=2)
+        for t in range(PACK):
+            nc.tensor.transpose(us_turn[:, t, :], us_cols[:, t : t + 1].to_broadcast([P, P]), ident[:])
+        us_rows = keep.tile([P, 2, P, 2], F32, name="us_rows")
+        nc.vector.tensor_copy(us_rows[:], us_turn[:].rearrange("m (u j) p -> m u p j", j=2))
 
         halves = range(2)
         u_grouped = [keep.tile([P, 2 * P * PACK], BF16, name="u_grouped%d" % h, align_bytes=64) for h in halves]
@@ -141,10 +147,13 @@ def tile_attend_at_txl_topk_kernel(tc, uT, pT, k_words, k_scales, c_words, c_sca
         weight_tile = keep.tile([P, Q_BLOCKS, PACK, P], F32, name="weights")
         weights = [weight_tile[:, qb] for qb in range(Q_BLOCKS)]
         for qb in range(Q_BLOCKS):
-            nc.scalar.activation(
-                weights[qb], scores[qb][:].rearrange("q (p t) -> q t p", t=PACK),
-                mybir.ActivationFunctionType.Exp, bias=neg_ls[:, qb : qb + 1],
-            )
+            if qb in (1, 2):
+                laid = weights[qb].rearrange("q t p -> q (t p)").rearrange("q (u p j) -> q u p j", u=2, j=2)
+                read = scores[qb][:].rearrange("q (p u j) -> q u p j", u=2, j=2)
+            else:
+                laid = weights[qb]
+                read = scores[qb][:].rearrange("q (p t) -> q t p", t=PACK)
+            nc.scalar.activation(laid, read, mybir.ActivationFunctionType.Exp, bias=neg_ls[:, qb : qb + 1])
 
         us_wide = us_cols[:].unsqueeze(1).to_broadcast([P, P, PACK])
         picked = [keep.tile([P, SLOTS], BF16, name="picked%d" % b) for b in range(V_BLOCKS)]
@@ -155,23 +164,34 @@ def tile_attend_at_txl_topk_kernel(tc, uT, pT, k_words, k_scales, c_words, c_sca
                 nc.tensor.transpose(turned[:, t, :], weights[qb][:, t, :], ident[:])
             nc.vector.tensor_tensor(grouped, turned[:].rearrange("p t q -> p q t"), us_wide, mybir.AluOpType.mult)
 
-        def scale_on_scalar(q_blocks):
-            y_pairs = keep.tile([P, 2, 2 * P, 2], BF16, name="y_pairs", align_bytes=64)
-            for i, qb in enumerate(q_blocks):
-                turned = psum.tile([P, PACK, P], F32, name="score%d" % i)
-                for t in range(PACK):
-                    nc.tensor.transpose(turned[:, t, :], weights[qb][:, t, :], ident[:])
-                for t in range(PACK):
-                    nc.scalar.activation(
-                        y_pairs[:, t // 2, i * P : (i + 1) * P, t % 2], turned[:, t, :],
-                        mybir.ActivationFunctionType.Copy, scale=us_cols[:, t : t + 1],
-                    )
-            grouped = keep.tile([P, 2 * P * PACK], BF16, name="y_grouped_mid", align_bytes=64)
+        def scale_on_scalar(qb, grouped):
+            y_pairs = keep.tile([P, 2, P, 2], BF16, name="y_pairs", align_bytes=64)
+            turned = psum.tile([P, PACK, P], F32, name="turn", bufs=2)
+            for t in range(PACK):
+                nc.tensor.transpose(turned[:, t, :], weights[qb][:, t, :], ident[:])
+            for t in range(PACK):
+                nc.scalar.activation(
+                    y_pairs[:, t // 2, :, t % 2], turned[:, t, :],
+                    mybir.ActivationFunctionType.Copy, scale=us_cols[:, t : t + 1],
+                )
             nc.scalar.copy(
-                grouped[:].bitcast(F32).rearrange("p (q u) -> p q u", u=2),
+                grouped.bitcast(F32).rearrange("p (q u) -> p q u", u=2),
                 y_pairs[:].rearrange("p u q j -> p (u q j)").bitcast(F32).rearrange("p (u q) -> p q u", u=2),
             )
-            return grouped[:]
+
+        def scale_on_gpsimd(qb, grouped):
+            scaled = keep.tile([P, SLOTS], BF16, name="scaled%d" % qb)
+            nc.gpsimd.tensor_tensor(
+                scaled[:], weights[qb].rearrange("q t p -> q (t p)"), us_rows[:].rearrange("q u p j -> q (u p j)"),
+                mybir.AluOpType.mult,
+            )
+            pairs = scaled[:].bitcast(F32)
+            turned = psum.tile([P, PACK, P], F32, name="score%d" % (qb + 1))
+            for u in range(2):
+                nc.tensor.transpose(turned[:, u, :], pairs[:, u * P : (u + 1) * P], ident[:])
+            nc.scalar.copy(
+                grouped.bitcast(F32).rearrange("p (q u) -> p q u", u=2), turned[:, 0:2, :].rearrange("p u q -> p q u")
+            )
 
         def gather_values(b):
             nc.vector.tensor_copy(picked[b][:], v_pool[b][:].indirect(tok_list[:]))
@@ -210,17 +230,19 @@ def tile_attend_at_txl_topk_kernel(tc, uT, pT, k_words, k_scales, c_words, c_sca
         v_back = keep.tile([P, 2, P * PACK], BF16, name="v_back", align_bytes=64)
         v_grouped = [v_front[:, 0], v_front[:, 1], v_back[:, 0], v_back[:, 1]]
         gather_values(0)
-        y_early = behind_gather(0, 0, [P, 2 * P, PACK], BF16, "y_early")
-        for qb in range(2):
-            scale_on_vector(qb, y_early[:, qb * P : (qb + 1) * P, :])
         turn_values(0)
-        y_late = scale_on_scalar((2, 3))
+        y_late = keep.tile([P, 2 * P * PACK], BF16, name="y_late", align_bytes=64)
+        y_early = behind_gather(0, 0, [P, 2 * P * PACK], BF16, "y_early")
+        scale_on_vector(0, y_early[:, 0 : P * PACK].rearrange("p (q t) -> p q t", t=PACK))
+        scale_on_gpsimd(1, y_early[:, P * PACK : 2 * P * PACK])
+        scale_on_scalar(3, y_late[:, P * PACK : 2 * P * PACK])
+        scale_on_gpsimd(2, y_late[:, 0 : P * PACK])
         gather_values(1)
         turn_values(1)
-        y01 = quantize("y01", y_early[:].rearrange("p q t -> p (q t)"), behind_gather(1, 0, [P, 2 * P], U32, "y01_codes")[:])
+        y01 = quantize("y01", y_early[:], behind_gather(1, 0, [P, 2 * P], U32, "y01_codes")[:])
         gather_values(2)
         turn_values(2)
-        y23 = quantize("y23", y_late, behind_gather(2, 1024, [P, 2 * P], U32, "y23_codes")[:])
+        y23 = quantize("y23", y_late[:], behind_gather(2, 1024, [P, 2 * P], U32, "y23_codes")[:])
         v01 = quantize(
             "v01", v_front[:].rearrange("p b x -> p (b x)"), behind_gather(2, 0, [P, 2 * P], U32, "v01_codes")[:]
         )

@@ -147,7 +147,7 @@ def tile_attend_at_txl_topk_kernel(tc, uT, pT, k_words, k_scales, c_words, c_sca
         weight_tile = keep.tile([P, Q_BLOCKS, PACK, P], F32, name="weights")
         weights = [weight_tile[:, qb] for qb in range(Q_BLOCKS)]
         for qb in range(Q_BLOCKS):
-            if qb in (1, 2):
+            if qb % 2 == 0:
                 laid = weights[qb].rearrange("q t p -> q (t p)").rearrange("q (u p j) -> q u p j", u=2, j=2)
                 read = scores[qb][:].rearrange("q (p u j) -> q u p j", u=2, j=2)
             else:
@@ -165,7 +165,7 @@ def tile_attend_at_txl_topk_kernel(tc, uT, pT, k_words, k_scales, c_words, c_sca
             nc.vector.tensor_tensor(grouped, turned[:].rearrange("p t q -> p q t"), us_wide, mybir.AluOpType.mult)
 
         def scale_on_scalar(qb, grouped):
-            y_pairs = keep.tile([P, 2, P, 2], BF16, name="y_pairs", align_bytes=64)
+            y_pairs = keep.tile([P, 2, P, 2], BF16, name="y_pairs", tag="scaled0")
             turned = psum.tile([P, PACK, P], F32, name="turn", bufs=2)
             for t in range(PACK):
                 nc.tensor.transpose(turned[:, t, :], weights[qb][:, t, :], ident[:])
@@ -179,14 +179,14 @@ def tile_attend_at_txl_topk_kernel(tc, uT, pT, k_words, k_scales, c_words, c_sca
                 y_pairs[:].rearrange("p u q j -> p (u q j)").bitcast(F32).rearrange("p (u q) -> p q u", u=2),
             )
 
-        def scale_on_gpsimd(qb, grouped):
+        def scale_on_gpsimd(qb, grouped, bank):
             scaled = keep.tile([P, SLOTS], BF16, name="scaled%d" % qb)
             nc.gpsimd.tensor_tensor(
                 scaled[:], weights[qb].rearrange("q t p -> q (t p)"), us_rows[:].rearrange("q u p j -> q (u p j)"),
                 mybir.AluOpType.mult,
             )
             pairs = scaled[:].bitcast(F32)
-            turned = psum.tile([P, PACK, P], F32, name="score%d" % (qb + 1))
+            turned = psum.tile([P, PACK, P], F32, name=bank)
             for u in range(2):
                 nc.tensor.transpose(turned[:, u, :], pairs[:, u * P : (u + 1) * P], ident[:])
             nc.scalar.copy(
@@ -196,9 +196,9 @@ def tile_attend_at_txl_topk_kernel(tc, uT, pT, k_words, k_scales, c_words, c_sca
         def gather_values(b):
             nc.vector.tensor_copy(picked[b][:], v_pool[b][:].indirect(tok_list[:]))
 
-        def turn_values(b):
+        def turn_values(b, bank="v_turn", bufs=2):
             pairs = picked[b][:].bitcast(F32)
-            turned = psum.tile([P, PACK, P], F32, name="v_turn", bufs=2)
+            turned = psum.tile([P, PACK, P], F32, name=bank, bufs=bufs)
             for u in range(2):
                 nc.tensor.transpose(turned[:, u, :], pairs[:, u : 2 * P : 2], ident[:])
             nc.scalar.copy(
@@ -230,22 +230,22 @@ def tile_attend_at_txl_topk_kernel(tc, uT, pT, k_words, k_scales, c_words, c_sca
         v_back = keep.tile([P, 2, P * PACK], BF16, name="v_back", align_bytes=64)
         v_grouped = [v_front[:, 0], v_front[:, 1], v_back[:, 0], v_back[:, 1]]
         gather_values(0)
-        turn_values(0)
         y_late = keep.tile([P, 2 * P * PACK], BF16, name="y_late", align_bytes=64)
         y_early = behind_gather(0, 0, [P, 2 * P * PACK], BF16, "y_early")
-        scale_on_vector(0, y_early[:, 0 : P * PACK].rearrange("p (q t) -> p q t", t=PACK))
-        scale_on_gpsimd(1, y_early[:, P * PACK : 2 * P * PACK])
+        scale_on_vector(1, y_early[:, P * PACK : 2 * P * PACK].rearrange("p (q t) -> p q t", t=PACK))
+        turn_values(0, "score1", 1)
+        scale_on_gpsimd(0, y_early[:, 0 : P * PACK], "score0")
         scale_on_scalar(3, y_late[:, P * PACK : 2 * P * PACK])
-        scale_on_gpsimd(2, y_late[:, 0 : P * PACK])
+        scale_on_gpsimd(2, y_late[:, 0 : P * PACK], "score3")
         gather_values(1)
         turn_values(1)
         y01 = quantize("y01", y_early[:], behind_gather(1, 0, [P, 2 * P], U32, "y01_codes")[:])
         gather_values(2)
         turn_values(2)
-        y23 = quantize("y23", y_late[:], behind_gather(2, 1024, [P, 2 * P], U32, "y23_codes")[:])
         v01 = quantize(
             "v01", v_front[:].rearrange("p b x -> p (b x)"), behind_gather(2, 0, [P, 2 * P], U32, "v01_codes")[:]
         )
+        y23 = quantize("y23", y_late[:], behind_gather(2, 1024, [P, 2 * P], U32, "y23_codes")[:])
         y_mx = [(y[0][:, i * P : (i + 1) * P], y[1][:, i * P : (i + 1) * P]) for y in (y01, y23) for i in range(2)]
         acc = psum.tile([P, 512], F32, name="turn", bufs=2)
         products(v01, (0, 1), acc)

@@ -119,11 +119,11 @@ def tile_attend_at_txl_topk_kernel(tc, uT, pT, k_words, k_scales, c_words, c_sca
         p_grouped = [keep.tile([P, 2 * P * PACK], BF16, name="p_grouped%d" % h, align_bytes=64) for h in halves]
         scores = [psum.tile([P, SLOTS], F32, name="score%d" % qb) for qb in range(Q_BLOCKS)]
 
-        def score_pass(qb, mx, codes, plane, first):
+        def score_pass(qb, mx, codes, plane, slots, start, stop):
             cols = slice(qb % 2 * P, (qb % 2 + 1) * P)
             nc.tensor.matmul_mx(
-                out=scores[qb][:], lhsT=mx[0][:, cols].bitcast(FP8X4), lhsT_scale=mx[1][:, cols],
-                rhs=codes[:].bitcast(FP8X4), rhs_scale=plane, start=first, stop=not first,
+                out=scores[qb][:, slots], lhsT=mx[0][:, cols].bitcast(FP8X4), lhsT_scale=mx[1][:, cols],
+                rhs=codes[:, slots].bitcast(FP8X4), rhs_scale=plane[:, slots], start=start, stop=stop,
             )
 
         for h in halves:
@@ -132,7 +132,7 @@ def tile_attend_at_txl_topk_kernel(tc, uT, pT, k_words, k_scales, c_words, c_sca
         def passes(name, h, grouped, codes, table_codes, plane, first):
             mx = quantize("%s%d" % (name, h), grouped[h][:], codes[:])
             for qb in (2 * h, 2 * h + 1):
-                score_pass(qb, mx, table_codes, plane, first)
+                score_pass(qb, mx, table_codes, plane, slice(0, SLOTS), first, not first)
 
         for h in halves:
             codes = behind_gather(V_BLOCKS + 1 - h, 0, [P, 256], U32, "p%d_codes" % h)
@@ -141,8 +141,12 @@ def tile_attend_at_txl_topk_kernel(tc, uT, pT, k_words, k_scales, c_words, c_sca
             interleave(nc.scalar.copy, u_grouped[h][:], u_raw[:, :, 256 * h : 256 * (h + 1)])
         neg_ls = keep.tile([P, Q_BLOCKS], F32, name="neg_ls", tag="u_raw")
         nc.scalar.mul(neg_ls[:], ls_turn[:, 0, 0:Q_BLOCKS], -1.0)
-        nc.vector.tensor_copy(k_codes[:], k_word_pool[:].bitcast(U32).indirect(tok_list[:]))
-        passes("u", 0, u_grouped, code_tile("u0", 256), k_codes, k_bytes[:], False)
+        u0 = quantize("u0", u_grouped[0][:], code_tile("u0", 256)[:])
+        for h in halves:
+            slots = slice(256 * h, 256 * (h + 1))
+            nc.vector.tensor_copy(k_codes[:, slots], k_word_pool[:].bitcast(U32).indirect(tok_list[:, 16 * h : 16 * (h + 1)]))
+            for qb in range(2):
+                score_pass(qb, u0, k_codes, k_bytes[:], slots, False, h == 1)
         passes("u", 1, u_grouped, behind_gather(V_BLOCKS + 2, 0, [P, 256], U32, "u1_codes"), k_codes, k_bytes[:], False)
         weight_tile = keep.tile([P, Q_BLOCKS, PACK, P], F32, name="weights")
         weights = [weight_tile[:, qb] for qb in range(Q_BLOCKS)]
@@ -150,10 +154,13 @@ def tile_attend_at_txl_topk_kernel(tc, uT, pT, k_words, k_scales, c_words, c_sca
             if qb % 2 == 0:
                 laid = weights[qb].rearrange("q t p -> q (t p)").rearrange("q (u p j) -> q u p j", u=2, j=2)
                 read = scores[qb][:].rearrange("q (p u j) -> q u p j", u=2, j=2)
+                parts = [(laid, read)]
             else:
-                laid = weights[qb]
                 read = scores[qb][:].rearrange("q (p t) -> q t p", t=PACK)
-            nc.scalar.activation(laid, read, mybir.ActivationFunctionType.Exp, bias=neg_ls[:, qb : qb + 1])
+                cuts = (0, 2, 4) if qb == 1 else (0, 4)
+                parts = [(weights[qb][:, a:b, :], read[:, a:b, :]) for a, b in zip(cuts, cuts[1:])]
+            for laid, read in parts:
+                nc.scalar.activation(laid, read, mybir.ActivationFunctionType.Exp, bias=neg_ls[:, qb : qb + 1])
 
         us_wide = us_cols[:].unsqueeze(1).to_broadcast([P, P, PACK])
         picked = [keep.tile([P, SLOTS], BF16, name="picked%d" % b) for b in range(V_BLOCKS)]

@@ -18,10 +18,16 @@ TOKENS = 2048
 DISTANCES = 1024
 QUERIES = 512
 VALUES = 512
+BANK = 512
 Q_BLOCKS = QUERIES // P
 V_BLOCKS = VALUES // P
-C_PLANE = 4
-POOL_BYTES = 4 * TOKENS
+HALF = 256
+GROUPED = P * PACK
+LIST_GROUP = 16
+C_FIRST_ROW = 4
+WINDOW_BYTES = 4 * TOKENS
+K_BYTES_AT, C_BYTES_AT, K_WORDS_AT = V_BLOCKS, V_BLOCKS + 1, V_BLOCKS + 2
+CODES_BYTES = 4 * HALF
 
 FLOPS = 3 * 2 * 512 * 512 * 512
 
@@ -30,26 +36,21 @@ def tile_attend_at_txl_topk_kernel(tc, uT, pT, k_words, k_scales, c_words, c_sca
     nc = tc.nc
     with ExitStack() as ctx:
         keep = ctx.enter_context(tc.tile_pool(name="keep", bufs=1))
-        values = ctx.enter_context(tc.tile_pool(name="values", bufs=1))
+        windows = ctx.enter_context(tc.tile_pool(name="values", bufs=1))
         psum = ctx.enter_context(tc.psum_pool(name="psum", bufs=1))
 
-        tok_list = keep.tile([P, SLOTS // 16], U16, name="tok_list")
-        dist_list = keep.tile([P, SLOTS // 16], U16, name="dist_list")
+        def on_window(window, start, shape, dtype, name):
+            return windows.tile(shape, dtype, name=name, align_bytes=64, offset=window * WINDOW_BYTES + start)
+
+        tok_list = keep.tile([P, SLOTS // LIST_GROUP], U16, name="tok_list")
+        dist_list = keep.tile([P, SLOTS // LIST_GROUP], U16, name="dist_list")
         c_word_pool = keep.tile([P, DISTANCES], I32, name="c_word_pool")
-        k_word_pool = values.tile([P, TOKENS], I32, name="k_word_pool", align_bytes=64, offset=(V_BLOCKS + 2) * POOL_BYTES)
-        c_byte_pool = values.tile(
-            [P, DISTANCES // 4], I32, name="c_byte_pool", align_bytes=64, offset=(V_BLOCKS + 1) * POOL_BYTES
-        )
-        k_byte_pool = values.tile([P, TOKENS // 4], I32, name="k_byte_pool", align_bytes=64, offset=V_BLOCKS * POOL_BYTES)
+        k_word_pool = on_window(K_WORDS_AT, 0, [P, TOKENS], I32, "k_word_pool")
+        c_byte_pool = on_window(C_BYTES_AT, 0, [P, DISTANCES // 4], I32, "c_byte_pool")
+        k_byte_pool = on_window(K_BYTES_AT, 0, [P, TOKENS // 4], I32, "k_byte_pool")
         u_raw = keep.tile([P, PACK, QUERIES], F32, name="u_raw")
         p_raw = keep.tile([P, PACK, QUERIES], F32, name="p_raw")
-        v_pool = [
-            values.tile([P, TOKENS], F32, name="v_pool%d" % b, align_bytes=64, offset=b * POOL_BYTES) for b in range(V_BLOCKS)
-        ]
-
-        def behind_gather(b, start, shape, dtype, name):
-            return values.tile(shape, dtype, name=name, align_bytes=64, offset=b * POOL_BYTES + start)
-
+        v_pool = [on_window(b, 0, [P, TOKENS], F32, "v_pool%d" % b) for b in range(V_BLOCKS)]
         ls_rows = keep.tile([P, P], F32, name="ls_rows")
         us_cols = keep.tile([P, PACK], F32, name="us_cols")
         ident = keep.tile([P, P], F32, name="ident")
@@ -59,25 +60,20 @@ def tile_attend_at_txl_topk_kernel(tc, uT, pT, k_words, k_scales, c_words, c_sca
         nc.gpsimd.memset(ls_rows[:], 0.0)
         make_identity(nc, ident[:])
 
-        def load_scale_rows(pool_tile, rows, first, r):
-            nc.sync.dma_start(pool_tile[first + r : P : 32, :], rows[0].bitcast(I32)[r:16:4, :])
-
         def words_of(x):
             return x[0].rearrange("p n t -> p (n t)").bitcast(I32)
+
+        def load_scale_rows(rows_in_quadrant):
+            for pool_tile, rows, first in ((c_byte_pool, c_scales, C_FIRST_ROW), (k_byte_pool, k_scales, 0)):
+                for r in rows_in_quadrant:
+                    nc.sync.dma_start(pool_tile[first + r : P : 32, :], rows[0].bitcast(I32)[r:16:4, :])
 
         nc.sync.dma_start(c_word_pool[:], words_of(c_words))
         nc.sync.dma_start(dist_list[:], offs2)
         nc.sync.dma_start(tok_list[:], offs)
-
-        def load_scale_rows_of_both(rows_in_quadrant):
-            for r in rows_in_quadrant:
-                load_scale_rows(c_byte_pool, c_scales, C_PLANE, r)
-            for r in rows_in_quadrant:
-                load_scale_rows(k_byte_pool, k_scales, 0, r)
-
-        load_scale_rows_of_both((0, 1))
+        load_scale_rows((0, 1))
         nc.sync.dma_start(p_raw[:], pT[0].rearrange("(p t) q -> p t q", t=PACK))
-        load_scale_rows_of_both((2, 3))
+        load_scale_rows((2, 3))
         nc.sync.dma_start(us_cols[:], us[0].rearrange("(p t) o -> p (t o)", t=PACK))
         nc.sync.dma_start(u_raw[:], uT[0].rearrange("(p t) q -> p t q", t=PACK))
         nc.sync.dma_start(k_word_pool[:], words_of(k_words))
@@ -93,96 +89,123 @@ def tile_attend_at_txl_topk_kernel(tc, uT, pT, k_words, k_scales, c_words, c_sca
         nc.vector.tensor_copy(c_bytes[:], c_byte_pool[:].bitcast(U8).indirect(dist_list[:]))
         nc.vector.tensor_copy(k_bytes[:], k_byte_pool[:].bitcast(U8).indirect(tok_list[:]))
 
-        def interleave(copy, grouped, raw):
+        def interleave(grouped, raw):
             src = raw.rearrange("p t (c i) -> p c t i", i=4)
-            copy(grouped.rearrange("p (c i t) -> p c t i", i=4, t=PACK), src)
+            nc.scalar.copy(grouped.rearrange("p (c i t) -> p c t i", i=4, t=PACK), src)
 
-        def code_tile(name, width, slot=""):
-            return keep.tile([P, width], U32, name=name + "_codes", tag=slot, align_bytes=64)
+        def code_tile(name, width):
+            return keep.tile([P, width], U32, name=name + "_codes", align_bytes=64)
 
         def quantize(name, grouped, codes):
             scales = keep.tile([P, codes.shape[1]], U8, name=name + "_scales", align_bytes=64)
             nc.vector.quantize_mx(out=codes.bitcast(FP8X4), scales=scales[:], in_=grouped)
             return codes, scales
 
-        ls_turn = psum.tile([P, PACK, P], F32, name="turn", bufs=2)
+        def turn_bank(shape):
+            return psum.tile(shape, F32, name="turn", bufs=2)
+
+        ls_turn = turn_bank([P, PACK, P])
         nc.tensor.transpose(ls_turn[:, 0, :], ls_rows[:], ident[:])
 
-        us_turn = psum.tile([P, PACK, P], F32, name="turn", bufs=2)
+        us_turn = turn_bank([P, PACK, P])
         for t in range(PACK):
             nc.tensor.transpose(us_turn[:, t, :], us_cols[:, t : t + 1].to_broadcast([P, P]), ident[:])
         us_rows = keep.tile([P, 2, P, 2], F32, name="us_rows")
         nc.vector.tensor_copy(us_rows[:], us_turn[:].rearrange("m (u j) p -> m u p j", j=2))
 
         halves = range(2)
-        u_grouped = [keep.tile([P, 2 * P * PACK], BF16, name="u_grouped%d" % h, align_bytes=64) for h in halves]
-        p_grouped = [keep.tile([P, 2 * P * PACK], BF16, name="p_grouped%d" % h, align_bytes=64) for h in halves]
-        scores = [psum.tile([P, SLOTS], F32, name="score%d" % qb) for qb in range(Q_BLOCKS)]
+        half_cols = [slice(HALF * h, HALF * (h + 1)) for h in halves]
+        u_grouped = [keep.tile([P, 2 * GROUPED], BF16, name="u_grouped%d" % h, align_bytes=64) for h in halves]
+        p_grouped = [keep.tile([P, 2 * GROUPED], BF16, name="p_grouped%d" % h, align_bytes=64) for h in halves]
+        score_banks = [psum.tile([P, BANK], F32, name="score%d" % i) for i in range(Q_BLOCKS)]
 
-        def score_pass(qb, mx, codes, plane, slots, start, stop):
+        def score_pass(acc, qb, queries_mx, codes, scale_rows, start, stop):
             cols = slice(qb % 2 * P, (qb % 2 + 1) * P)
             nc.tensor.matmul_mx(
-                out=scores[qb][:, slots], lhsT=mx[0][:, cols].bitcast(FP8X4), lhsT_scale=mx[1][:, cols],
-                rhs=codes[:, slots].bitcast(FP8X4), rhs_scale=plane[:, slots], start=start, stop=stop,
+                out=acc, lhsT=queries_mx[0][:, cols].bitcast(FP8X4), lhsT_scale=queries_mx[1][:, cols],
+                rhs=codes.bitcast(FP8X4), rhs_scale=scale_rows, start=start, stop=stop,
             )
 
-        for h in halves:
-            interleave(nc.scalar.copy, p_grouped[h][:], p_raw[:, :, 256 * h : 256 * (h + 1)])
-
-        def passes(name, h, grouped, codes, table_codes, plane, first):
-            mx = quantize("%s%d" % (name, h), grouped[h][:], codes[:])
-            for qb in (2 * h, 2 * h + 1):
-                score_pass(qb, mx, table_codes, plane, slice(0, SLOTS), first, not first)
+        def early_scores(qb, h):
+            return score_banks[h][:, half_cols[qb]]
 
         for h in halves:
-            codes = behind_gather(V_BLOCKS + 1 - h, 0, [P, 256], U32, "p%d_codes" % h)
-            passes("p", h, p_grouped, codes, c_codes, c_bytes[C_PLANE:P, :], True)
+            interleave(p_grouped[h][:], p_raw[:, :, half_cols[h]])
+        p0 = quantize("p0", p_grouped[0][:], on_window(C_BYTES_AT, 0, [P, HALF], U32, "p0_codes")[:])
+        for qb in (0, 1):
+            for h in halves:
+                slots = half_cols[h]
+                score_pass(early_scores(qb, h), qb, p0, c_codes[:, slots], c_bytes[C_FIRST_ROW:P, slots], qb == 0, False)
+        p1 = quantize("p1", p_grouped[1][:], on_window(K_BYTES_AT, 0, [P, HALF], U32, "p1_codes")[:])
+        for qb in (2, 3):
+            score_pass(score_banks[qb][:], qb, p1, c_codes[:], c_bytes[C_FIRST_ROW:P, :], True, False)
+
         for h in halves:
-            interleave(nc.scalar.copy, u_grouped[h][:], u_raw[:, :, 256 * h : 256 * (h + 1)])
+            interleave(u_grouped[h][:], u_raw[:, :, half_cols[h]])
         neg_ls = keep.tile([P, Q_BLOCKS], F32, name="neg_ls", tag="u_raw")
         nc.scalar.mul(neg_ls[:], ls_turn[:, 0, 0:Q_BLOCKS], -1.0)
-        u0 = quantize("u0", u_grouped[0][:], code_tile("u0", 256)[:])
+        u0 = quantize("u0", u_grouped[0][:], code_tile("u0", HALF)[:])
         for h in halves:
-            slots = slice(256 * h, 256 * (h + 1))
-            nc.vector.tensor_copy(k_codes[:, slots], k_word_pool[:].bitcast(U32).indirect(tok_list[:, 16 * h : 16 * (h + 1)]))
-            for qb in range(2):
-                score_pass(qb, u0, k_codes, k_bytes[:], slots, False, h == 1)
-        passes("u", 1, u_grouped, behind_gather(V_BLOCKS + 2, 0, [P, 256], U32, "u1_codes"), k_codes, k_bytes[:], False)
+            slots = half_cols[h]
+            entries = tok_list[:, slots.start // LIST_GROUP : slots.stop // LIST_GROUP]
+            nc.vector.tensor_copy(k_codes[:, slots], k_word_pool[:].bitcast(U32).indirect(entries))
+            for qb in (0, 1):
+                score_pass(early_scores(qb, h), qb, u0, k_codes[:, slots], k_bytes[:, slots], False, qb == 1)
+        u1 = quantize("u1", u_grouped[1][:], on_window(K_WORDS_AT, 0, [P, HALF], U32, "u1_codes")[:])
+        for qb in (2, 3):
+            score_pass(score_banks[qb][:], qb, u1, k_codes[:], k_bytes[:], False, True)
+
         weight_tile = keep.tile([P, Q_BLOCKS, PACK, P], F32, name="weights")
         weights = [weight_tile[:, qb] for qb in range(Q_BLOCKS)]
-        for qb in range(Q_BLOCKS):
-            if qb % 2 == 0:
-                laid = weights[qb].rearrange("q t p -> q (t p)").rearrange("q (u p j) -> q u p j", u=2, j=2)
-                read = scores[qb][:].rearrange("q (p u j) -> q u p j", u=2, j=2)
-                parts = [(laid, read)]
-            else:
-                read = scores[qb][:].rearrange("q (p t) -> q t p", t=PACK)
-                cuts = (0, 2, 4) if qb == 1 else (0, 4)
-                parts = [(weights[qb][:, a:b, :], read[:, a:b, :]) for a, b in zip(cuts, cuts[1:])]
-            for laid, read in parts:
-                nc.scalar.activation(laid, read, mybir.ActivationFunctionType.Exp, bias=neg_ls[:, qb : qb + 1])
+
+        def exponential(qb, laid, read):
+            nc.scalar.activation(laid, read, mybir.ActivationFunctionType.Exp, bias=neg_ls[:, qb : qb + 1])
+
+        def laid_by_pairs(qb):
+            return weights[qb].rearrange("q t p -> q (t p)").rearrange("q (u p j) -> q u p j", u=2, j=2)
+
+        def read_by_pairs(scores):
+            return scores.rearrange("q (p u j) -> q u p j", u=2, j=2)
+
+        def read_by_places(scores):
+            return scores.rearrange("q (p t) -> q t p", t=PACK)
+
+        for h in halves:
+            p_range = slice(HALF // PACK * h, HALF // PACK * (h + 1))
+            exponential(0, laid_by_pairs(0)[:, :, p_range, :], read_by_pairs(early_scores(0, h)))
+            exponential(1, weights[1][:, :, p_range], read_by_places(early_scores(1, h)))
+        exponential(2, laid_by_pairs(2), read_by_pairs(score_banks[2][:]))
+        for u in range(2):
+            places = slice(2 * u, 2 * u + 2)
+            exponential(3, weights[3][:, places, :], read_by_places(score_banks[3][:])[:, places, :])
 
         us_wide = us_cols[:].unsqueeze(1).to_broadcast([P, P, PACK])
         picked = [keep.tile([P, SLOTS], BF16, name="picked%d" % b) for b in range(V_BLOCKS)]
 
+        def as_pairs(grouped):
+            return grouped.bitcast(F32).rearrange("p (c u) -> p c u", u=2)
+
         def scale_on_vector(qb, grouped):
-            turned = psum.tile([P, PACK, P], F32, name="turn", bufs=2)
+            turned = turn_bank([P, PACK, P])
             for t in range(PACK):
                 nc.tensor.transpose(turned[:, t, :], weights[qb][:, t, :], ident[:])
-            nc.vector.tensor_tensor(grouped, turned[:].rearrange("p t q -> p q t"), us_wide, mybir.AluOpType.mult)
+            nc.vector.tensor_tensor(
+                grouped.rearrange("p (q t) -> p q t", t=PACK), turned[:].rearrange("p t q -> p q t"), us_wide,
+                mybir.AluOpType.mult,
+            )
 
         def scale_on_scalar(qb, grouped):
             y_pairs = keep.tile([P, 2, P, 2], BF16, name="y_pairs", tag="scaled0")
-            turned = psum.tile([P, PACK, P], F32, name="turn", bufs=2)
+            banks = [turn_bank([P, 2, P]), psum.tile([P, 2, P], F32, name="score2")]
             for t in range(PACK):
-                nc.tensor.transpose(turned[:, t, :], weights[qb][:, t, :], ident[:])
+                nc.tensor.transpose(banks[t // 2][:, t % 2, :], weights[qb][:, t, :], ident[:])
             for t in range(PACK):
                 nc.scalar.activation(
-                    y_pairs[:, t // 2, :, t % 2], turned[:, t, :],
+                    y_pairs[:, t // 2, :, t % 2], banks[t // 2][:, t % 2, :],
                     mybir.ActivationFunctionType.Copy, scale=us_cols[:, t : t + 1],
                 )
             nc.scalar.copy(
-                grouped.bitcast(F32).rearrange("p (q u) -> p q u", u=2),
+                as_pairs(grouped),
                 y_pairs[:].rearrange("p u q j -> p (u q j)").bitcast(F32).rearrange("p (u q) -> p q u", u=2),
             )
 
@@ -196,22 +219,19 @@ def tile_attend_at_txl_topk_kernel(tc, uT, pT, k_words, k_scales, c_words, c_sca
             turned = psum.tile([P, PACK, P], F32, name=bank)
             for u in range(2):
                 nc.tensor.transpose(turned[:, u, :], pairs[:, u * P : (u + 1) * P], ident[:])
-            nc.scalar.copy(
-                grouped.bitcast(F32).rearrange("p (q u) -> p q u", u=2), turned[:, 0:2, :].rearrange("p u q -> p q u")
-            )
+            nc.scalar.copy(as_pairs(grouped), turned[:, 0:2, :].rearrange("p u q -> p q u"))
 
         def gather_values(b):
             nc.vector.tensor_copy(picked[b][:], v_pool[b][:].indirect(tok_list[:]))
 
-        def turn_values(b, bank="v_turn", bufs=2):
+        def value_bank(shape):
+            return psum.tile(shape, F32, name="v_turn", bufs=2)
+
+        def turn_values(b, turned):
             pairs = picked[b][:].bitcast(F32)
-            turned = psum.tile([P, PACK, P], F32, name=bank, bufs=bufs)
             for u in range(2):
                 nc.tensor.transpose(turned[:, u, :], pairs[:, u : 2 * P : 2], ident[:])
-            nc.scalar.copy(
-                v_grouped[b].bitcast(F32).rearrange("p (e u) -> p e u", u=2),
-                turned[:, 0:2, :].rearrange("p u e -> p e u"),
-            )
+            nc.scalar.copy(as_pairs(v_grouped[b]), turned[:, 0:2, :].rearrange("p u e -> p e u"))
 
         out_rows = out[0].rearrange("(b q) e -> q b e", q=P)
 
@@ -221,60 +241,69 @@ def tile_attend_at_txl_topk_kernel(tc, uT, pT, k_words, k_scales, c_words, c_sca
                 rhs=v_mx[0].bitcast(FP8X4), rhs_scale=v_mx[1][:], start=True, stop=True,
             )
 
-        def products(v_mx, q_blocks, acc):
+        def products_out(v_mx, first_feature, q_blocks, acc, staged):
             width = v_mx[0].shape[1]
             for i, qb in enumerate(q_blocks):
                 product(acc[:, i * width : (i + 1) * width], qb, v_mx)
-
-        def empty(acc, first_block, width, q_blocks, copy, staged):
-            copy(staged[:], acc[:, 0 : len(q_blocks) * width])
+            nc.scalar.copy(staged[:], acc[:, 0 : len(q_blocks) * width])
             nc.sync.dma_start(
-                out_rows[:, q_blocks[0] : q_blocks[-1] + 1, first_block * P : first_block * P + width],
+                out_rows[:, q_blocks[0] : q_blocks[-1] + 1, first_feature : first_feature + width],
                 staged[:].rearrange("q (b e) -> q b e", e=width),
             )
 
-        v_front = keep.tile([P, 2, P * PACK], BF16, name="v_front", align_bytes=64)
-        v_back = keep.tile([P, 2, P * PACK], BF16, name="v_back", align_bytes=64)
+        v_front = keep.tile([P, 2, GROUPED], BF16, name="v_front", align_bytes=64)
+        v_back = keep.tile([P, 2, GROUPED], BF16, name="v_back", align_bytes=64)
         v_grouped = [v_front[:, 0], v_front[:, 1], v_back[:, 0], v_back[:, 1]]
+        first, second = slice(0, GROUPED), slice(GROUPED, 2 * GROUPED)
+
         gather_values(0)
-        y_late = keep.tile([P, 2 * P * PACK], BF16, name="y_late", align_bytes=64)
-        y_early = behind_gather(0, 0, [P, 2 * P * PACK], BF16, "y_early")
-        scale_on_vector(1, y_early[:, P * PACK : 2 * P * PACK].rearrange("p (q t) -> p q t", t=PACK))
-        turn_values(0, "score1", 1)
-        scale_on_gpsimd(0, y_early[:, 0 : P * PACK], "score0")
-        scale_on_scalar(3, y_late[:, P * PACK : 2 * P * PACK])
-        scale_on_gpsimd(2, y_late[:, 0 : P * PACK], "score3")
+        y_late = keep.tile([P, 2 * GROUPED], BF16, name="y_late", align_bytes=64)
+        y_early = on_window(0, 0, [P, 2 * GROUPED], BF16, "y_early")
+        scale_on_vector(1, y_early[:, second])
+        turn_values(0, psum.tile([P, PACK, P], F32, name="score1"))
+        scale_on_gpsimd(0, y_early[:, first], "score0")
+        scale_on_scalar(3, y_late[:, second])
+        scale_on_gpsimd(2, y_late[:, first], "score3")
         gather_values(1)
-        turn_values(1)
-        y01 = quantize("y01", y_early[:], behind_gather(1, 0, [P, 2 * P], U32, "y01_codes")[:])
+        turn_values(1, value_bank([P, PACK, P]))
+        y01 = quantize("y01", y_early[:], on_window(1, 0, [P, HALF], U32, "y01_codes")[:])
+        v01_codes = on_window(2, -CODES_BYTES // 2, [P, 2 * P], U32, "v01_codes")
+        v01_scales = keep.tile([P, 2 * P], U8, name="v01_scales", align_bytes=64)
+        v01 = (v01_codes[:], v01_scales)
+
+        def quantize_front_values(b):
+            cols = slice(b * P, (b + 1) * P)
+            nc.vector.quantize_mx(out=v01_codes[:, cols].bitcast(FP8X4), scales=v01_scales[:, cols], in_=v_grouped[b])
+
+        quantize_front_values(0)
         gather_values(2)
-        turn_values(2)
-        v01 = quantize(
-            "v01", v_front[:].rearrange("p b x -> p (b x)"), behind_gather(2, 0, [P, 2 * P], U32, "v01_codes")[:]
-        )
-        y23 = quantize("y23", y_late[:], behind_gather(2, 1024, [P, 2 * P], U32, "y23_codes")[:])
+        turn_values(2, value_bank([P, PACK, P]))
+        quantize_front_values(1)
+        y23 = quantize("y23", y_late[:], on_window(2, CODES_BYTES, [P, HALF], U32, "y23_codes")[:])
         y_mx = [(y[0][:, i * P : (i + 1) * P], y[1][:, i * P : (i + 1) * P]) for y in (y01, y23) for i in range(2)]
-        acc = psum.tile([P, 512], F32, name="turn", bufs=2)
-        products(v01, (0, 1), acc)
-        empty(acc, 0, 2 * P, (0, 1), nc.scalar.copy, keep.tile([P, 512], F32, name="front0"))
-        front_banks = [psum.tile([P, 512], F32, name="turn", bufs=2), psum.tile([P, 512], F32, name="score3")]
+
+        products_out(v01, 0, (0, 1), turn_bank([P, BANK]), keep.tile([P, 2 * HALF], F32, name="front0"))
+        front_banks = [turn_bank([P, BANK]), psum.tile([P, BANK], F32, name="score3")]
         for i in range(2):
-            products(v01, (2 + i,), front_banks[i])
+            product(front_banks[i][:, 0 : 2 * P], 2 + i, v01)
         gather_values(3)
-        front_late = behind_gather(3, 1024, [P, 2, 2 * P], F32, "front_late")
+        front_late = on_window(3, CODES_BYTES, [P, 2, 2 * P], F32, "front_late")
         nc.scalar.copy(front_late[:, 0], front_banks[0][:, 0 : 2 * P])
-        turn_values(3)
-        v2 = quantize("v2", v_grouped[2], behind_gather(3, 0, [P, P], U32, "v2_codes")[:])
+        turn_values(3, value_bank([P, PACK, P]))
+        v2 = quantize("v2", v_grouped[2], on_window(3, 0, [P, P], U32, "v2_codes")[:])
         nc.vector.tensor_copy(front_late[:, 1], front_banks[1][:, 0 : 2 * P])
         nc.sync.dma_start(out_rows[:, 2:4, 0 : 2 * P], front_late[:])
         v3 = quantize("v3", v_grouped[3], code_tile("v3", P)[:])
-        for h in halves:
-            acc = psum.tile([P, 512], F32, name=("score2", "v_turn")[h], bufs=(1, 2)[h])
-            products(v2, (2 * h, 2 * h + 1), acc)
-            empty(acc, 2, P, (2 * h, 2 * h + 1), nc.scalar.copy, keep.tile([P, 256], F32, name="third%d" % h))
-        last_staged = [keep.tile([P, 2, P], F32, name="last%d" % e) for e in range(2)]
+
+        products_out(v2, 2 * P, (0, 1), psum.tile([P, BANK], F32, name="score2"), keep.tile([P, 2 * P], F32, name="third0"))
+        products_out(v2, 2 * P, (2, 3), value_bank([P, BANK]), keep.tile([P, 2 * P], F32, name="third1"))
+
+        last_staged = [keep.tile([P, 2, P], F32, name="last%d" % h) for h in halves]
         for qb in range(Q_BLOCKS):
-            acc = psum.tile([P, 512], F32, name=("score3", "score0", "score1", "turn")[qb], bufs=(1, 1, 1, 2)[qb])
+            if qb < Q_BLOCKS - 1:
+                acc = psum.tile([P, BANK], F32, name="score%d" % ((qb - 1) % Q_BLOCKS))
+            else:
+                acc = turn_bank([P, BANK])
             product(acc[:, 0:P], qb, v3)
             (nc.vector.tensor_copy, nc.scalar.copy)[qb // 2](last_staged[qb // 2][:, qb % 2, :], acc[:, 0:P])
         nc.sync.dma_start(out_rows[:, 0:2, 3 * P : 4 * P], last_staged[0][:])

@@ -28,6 +28,7 @@ C_FIRST_ROW = 4
 WINDOW_BYTES = 4 * TOKENS
 K_BYTES_AT, C_BYTES_AT, K_WORDS_AT = V_BLOCKS, V_BLOCKS + 1, V_BLOCKS + 2
 CODES_BYTES = 4 * HALF
+VECTOR_SLOTS = 320
 
 FLOPS = 3 * 2 * 512 * 512 * 512
 
@@ -221,8 +222,12 @@ def tile_attend_at_txl_topk_kernel(tc, uT, pT, k_words, k_scales, c_words, c_sca
                 nc.tensor.transpose(turned[:, u, :], pairs[:, u * P : (u + 1) * P], ident[:])
             nc.scalar.copy(as_pairs(grouped), turned[:, 0:2, :].rearrange("p u q -> p q u"))
 
-        def gather_values(b):
-            nc.vector.tensor_copy(picked[b][:], v_pool[b][:].indirect(tok_list[:]))
+        def gather_values(b, split=SLOTS):
+            column = split // LIST_GROUP
+            nc.vector.tensor_copy(picked[b][:, 0:split], v_pool[b][:].indirect(tok_list[:, 0:column]))
+            if split < SLOTS:
+                window = v_pool[b][:].indirect(tok_list[:, column : SLOTS // LIST_GROUP])
+                nc.scalar.activation(picked[b][:, split:SLOTS], window, mybir.ActivationFunctionType.Copy)
 
         def value_bank(shape):
             return psum.tile(shape, F32, name="v_turn", bufs=2)
@@ -282,17 +287,17 @@ def tile_attend_at_txl_topk_kernel(tc, uT, pT, k_words, k_scales, c_words, c_sca
         y23 = quantize("y23", y_late[:], on_window(2, CODES_BYTES, [P, HALF], U32, "y23_codes")[:])
         y_mx = [(y[0][:, i * P : (i + 1) * P], y[1][:, i * P : (i + 1) * P]) for y in (y01, y23) for i in range(2)]
 
-        products_out(v01, 0, (0, 1), turn_bank([P, BANK]), keep.tile([P, 2 * HALF], F32, name="front0"))
-        front_banks = [turn_bank([P, BANK]), psum.tile([P, BANK], F32, name="score3")]
-        for i in range(2):
-            product(front_banks[i][:, 0 : 2 * P], 2 + i, v01)
-        gather_values(3)
-        front_late = on_window(3, CODES_BYTES, [P, 2, 2 * P], F32, "front_late")
-        nc.scalar.copy(front_late[:, 0], front_banks[0][:, 0 : 2 * P])
-        turn_values(3, value_bank([P, PACK, P]))
+        front_banks = [turn_bank([P, BANK]), turn_bank([P, BANK])]
+        for qb in range(Q_BLOCKS):
+            product(front_banks[qb // 2][:, qb % 2 * HALF : (qb % 2 + 1) * HALF], qb, v01)
+        gather_values(3, VECTOR_SLOTS)
         v2 = quantize("v2", v_grouped[2], on_window(3, 0, [P, P], U32, "v2_codes")[:])
-        nc.vector.tensor_copy(front_late[:, 1], front_banks[1][:, 0 : 2 * P])
-        nc.sync.dma_start(out_rows[:, 2:4, 0 : 2 * P], front_late[:])
+        front = on_window(3, CODES_BYTES, [P, Q_BLOCKS, HALF], F32, "front")
+        nc.scalar.copy(front[:, 0:2, :], front_banks[0][:].rearrange("q (b e) -> q b e", b=2))
+        nc.sync.dma_start(out_rows[:, 0:2, 0:HALF], front[:, 0:2, :])
+        nc.vector.tensor_copy(front[:, 2:4, :], front_banks[1][:].rearrange("q (b e) -> q b e", b=2))
+        nc.sync.dma_start(out_rows[:, 2:4, 0:HALF], front[:, 2:4, :])
+        turn_values(3, value_bank([P, PACK, P]))
         v3 = quantize("v3", v_grouped[3], code_tile("v3", P)[:])
 
         products_out(v2, 2 * P, (0, 1), psum.tile([P, BANK], F32, name="score2"), keep.tile([P, 2 * P], F32, name="third0"))

@@ -56,39 +56,46 @@ def tile_attend_at_txl_topk_kernel(tc, uT, pT, k_words, k_scales, c_words, c_sca
         us_cols = keep.tile([P, PACK], F32, name="us_cols")
         ident = keep.tile([P, P], F32, name="ident")
 
-        nc.gpsimd.memset(c_byte_pool[:], 0)
         nc.gpsimd.memset(k_byte_pool[:], 0)
+        nc.gpsimd.memset(c_byte_pool[:], 0)
         nc.gpsimd.memset(ls_rows[:], 0.0)
         make_identity(nc, ident[:])
 
         def words_of(x):
             return x[0].rearrange("p n t -> p (n t)").bitcast(I32)
 
-        def load_scale_rows(rows_in_quadrant):
-            for pool_tile, rows, first in ((c_byte_pool, c_scales, C_FIRST_ROW), (k_byte_pool, k_scales, 0)):
-                for r in rows_in_quadrant:
-                    nc.sync.dma_start(pool_tile[first + r : P : 32, :], rows[0].bitcast(I32)[r:16:4, :])
+        def load_position_rows(rows_in_quadrant):
+            for r in rows_in_quadrant:
+                nc.sync.dma_start(c_byte_pool[C_FIRST_ROW + r : P : 32, :], c_scales[0].bitcast(I32)[r:16:4, :])
 
         nc.sync.dma_start(c_word_pool[:], words_of(c_words))
-        nc.sync.dma_start(dist_list[:], offs2)
         nc.sync.dma_start(tok_list[:], offs)
-        load_scale_rows((0, 1))
+        nc.sync.dma_start(k_byte_pool[0:P:8, :], k_scales[0].bitcast(I32))
+        nc.sync.dma_start(dist_list[:], offs2)
+        load_position_rows((0, 1))
         nc.sync.dma_start(p_raw[:], pT[0].rearrange("(p t) q -> p t q", t=PACK))
-        load_scale_rows((2, 3))
+        load_position_rows((2, 3))
         nc.sync.dma_start(us_cols[:], us[0].rearrange("(p t) o -> p (t o)", t=PACK))
         nc.sync.dma_start(u_raw[:], uT[0].rearrange("(p t) q -> p t q", t=PACK))
-        nc.sync.dma_start(k_word_pool[:], words_of(k_words))
         nc.gpsimd.dma_start(ls_rows[0:Q_BLOCKS, :], ls[0].rearrange("o (b m) -> (o b) m", m=P))
+
+        k_picked = keep.tile([P, SLOTS], U8, name="k_picked", align_bytes=64)
+        k_plane = keep.tile([P, SLOTS // 4], I32, name="k_plane", align_bytes=64)
+        nc.vector.tensor_copy(k_picked[:], k_byte_pool[:].bitcast(U8).indirect(tok_list[:]))
+        nc.vector.tensor_copy(k_plane[:], k_picked[:].bitcast(I32))
+        for r in (1, 2, 3):
+            nc.sync.dma_start(k_plane[r:P:32, :], k_picked[:].bitcast(I32)[8 * r : P : 32, :])
+        k_bytes = k_plane[:].bitcast(U8)
+        nc.sync.dma_start(k_word_pool[:], words_of(k_words))
         for b in range(V_BLOCKS):
             nc.sync.dma_start(v_pool[b][:], vT[b * P : (b + 1) * P, :])
 
-        c_codes = keep.tile([P, SLOTS], U32, name="c_codes", align_bytes=64)
-        c_bytes = keep.tile([P, SLOTS], U8, name="c_bytes", align_bytes=64)
+        c_codes = on_window(K_BYTES_AT, 0, [P, SLOTS], U32, "c_codes")
+        c_picked = keep.tile([P, SLOTS], U8, name="c_picked", align_bytes=64)
         k_codes = keep.tile([P, SLOTS], U32, name="k_codes", align_bytes=64)
-        k_bytes = keep.tile([P, SLOTS], U8, name="k_bytes", align_bytes=64)
         nc.vector.tensor_copy(c_codes[:], c_word_pool[:].bitcast(U32).indirect(dist_list[:]))
-        nc.vector.tensor_copy(c_bytes[:], c_byte_pool[:].bitcast(U8).indirect(dist_list[:]))
-        nc.vector.tensor_copy(k_bytes[:], k_byte_pool[:].bitcast(U8).indirect(tok_list[:]))
+        nc.vector.tensor_copy(c_picked[:], c_byte_pool[:].bitcast(U8).indirect(dist_list[:]))
+        c_bytes = c_picked[C_FIRST_ROW:P, :]
 
         def interleave(grouped, raw):
             src = raw.rearrange("p t (c i) -> p c t i", i=4)
@@ -105,14 +112,14 @@ def tile_attend_at_txl_topk_kernel(tc, uT, pT, k_words, k_scales, c_words, c_sca
         def turn_bank(shape):
             return psum.tile(shape, F32, name="turn", bufs=2)
 
-        ls_turn = turn_bank([P, PACK, P])
-        nc.tensor.transpose(ls_turn[:, 0, :], ls_rows[:], ident[:])
-
         us_turn = turn_bank([P, PACK, P])
         for t in range(PACK):
             nc.tensor.transpose(us_turn[:, t, :], us_cols[:, t : t + 1].to_broadcast([P, P]), ident[:])
         us_rows = keep.tile([P, 2, P, 2], F32, name="us_rows")
-        nc.vector.tensor_copy(us_rows[:], us_turn[:].rearrange("m (u j) p -> m u p j", j=2))
+        nc.scalar.copy(us_rows[:], us_turn[:].rearrange("m (u j) p -> m u p j", j=2))
+
+        ls_turn = turn_bank([P, PACK, P])
+        nc.tensor.transpose(ls_turn[:, 0, :], ls_rows[:], ident[:])
 
         halves = range(2)
         half_cols = [slice(HALF * h, HALF * (h + 1)) for h in halves]
@@ -136,10 +143,10 @@ def tile_attend_at_txl_topk_kernel(tc, uT, pT, k_words, k_scales, c_words, c_sca
         for qb in (0, 1):
             for h in halves:
                 slots = half_cols[h]
-                score_pass(early_scores(qb, h), qb, p0, c_codes[:, slots], c_bytes[C_FIRST_ROW:P, slots], qb == 0, False)
-        p1 = quantize("p1", p_grouped[1][:], on_window(K_BYTES_AT, 0, [P, HALF], U32, "p1_codes")[:])
+                score_pass(early_scores(qb, h), qb, p0, c_codes[:, slots], c_bytes[:, slots], qb == 0, False)
+        p1 = quantize("p1", p_grouped[1][:], code_tile("p1", HALF)[:])
         for qb in (2, 3):
-            score_pass(score_banks[qb][:], qb, p1, c_codes[:], c_bytes[C_FIRST_ROW:P, :], True, False)
+            score_pass(score_banks[qb][:], qb, p1, c_codes[:], c_bytes, True, False)
 
         for h in halves:
             interleave(u_grouped[h][:], u_raw[:, :, half_cols[h]])
@@ -154,7 +161,7 @@ def tile_attend_at_txl_topk_kernel(tc, uT, pT, k_words, k_scales, c_words, c_sca
                 score_pass(early_scores(qb, h), qb, u0, k_codes[:, slots], k_bytes[:, slots], False, qb == 1)
         u1 = quantize("u1", u_grouped[1][:], on_window(K_WORDS_AT, 0, [P, HALF], U32, "u1_codes")[:])
         for qb in (2, 3):
-            score_pass(score_banks[qb][:], qb, u1, k_codes[:], k_bytes[:], False, True)
+            score_pass(score_banks[qb][:], qb, u1, k_codes[:], k_bytes, False, True)
 
         weight_tile = keep.tile([P, Q_BLOCKS, PACK, P], F32, name="weights")
         weights = [weight_tile[:, qb] for qb in range(Q_BLOCKS)]

@@ -77,6 +77,7 @@ def tile_attend_at_txl_topk_kernel(tc, uT, pT, k_words, k_scales, c_words, c_sca
         load_position_rows((2, 3))
         nc.sync.dma_start(us_cols[:], us[0].rearrange("(p t) o -> p (t o)", t=PACK))
         nc.sync.dma_start(u_raw[:], uT[0].rearrange("(p t) q -> p t q", t=PACK))
+        nc.sync.dma_start(k_word_pool[:], words_of(k_words))
         nc.gpsimd.dma_start(ls_rows[0:Q_BLOCKS, :], ls[0].rearrange("o (b m) -> (o b) m", m=P))
 
         k_picked = keep.tile([P, SLOTS], U8, name="k_picked", align_bytes=64)
@@ -86,7 +87,6 @@ def tile_attend_at_txl_topk_kernel(tc, uT, pT, k_words, k_scales, c_words, c_sca
         for r in (1, 2, 3):
             nc.sync.dma_start(k_plane[r:P:32, :], k_picked[:].bitcast(I32)[8 * r : P : 32, :])
         k_bytes = k_plane[:].bitcast(U8)
-        nc.sync.dma_start(k_word_pool[:], words_of(k_words))
         for b in range(V_BLOCKS):
             nc.sync.dma_start(v_pool[b][:], vT[b * P : (b + 1) * P, :])
 

@@ -70,11 +70,10 @@ def tile_attend_at_txl_topk_kernel(tc, uT, pT, k_words, k_scales, c_words, c_sca
 
         nc.sync.dma_start(c_word_pool[:], words_of(c_words))
         nc.sync.dma_start(tok_list[:], offs)
-        nc.sync.dma_start(k_byte_pool[0:P:8, :], k_scales[0].bitcast(I32))
         nc.sync.dma_start(dist_list[:], offs2)
-        load_position_rows((0, 1))
+        nc.sync.dma_start(k_byte_pool[0:P:8, :], k_scales[0].bitcast(I32))
         nc.sync.dma_start(p_raw[:], pT[0].rearrange("(p t) q -> p t q", t=PACK))
-        load_position_rows((2, 3))
+        load_position_rows(range(4))
         nc.sync.dma_start(us_cols[:], us[0].rearrange("(p t) o -> p (t o)", t=PACK))
         nc.sync.dma_start(u_raw[:], uT[0].rearrange("(p t) q -> p t q", t=PACK))
         nc.sync.dma_start(k_word_pool[:], words_of(k_words))

@@ -28,7 +28,7 @@ C_FIRST_ROW = 4
 WINDOW_BYTES = 4 * TOKENS
 K_BYTES_AT, C_BYTES_AT, K_WORDS_AT = V_BLOCKS, V_BLOCKS + 1, V_BLOCKS + 2
 CODES_BYTES = 4 * HALF
-VECTOR_SLOTS = 320
+VECTOR_SLOTS = 288
 
 FLOPS = 3 * 2 * 512 * 512 * 512
 
@@ -287,7 +287,7 @@ def tile_attend_at_txl_topk_kernel(tc, uT, pT, k_words, k_scales, c_words, c_sca
             nc.vector.quantize_mx(out=v01_codes[:, cols].bitcast(FP8X4), scales=v01_scales[:, cols], in_=v_grouped[b])
 
         quantize_front_values(0)
-        gather_values(2)
+        gather_values(2, 384)
         turn_values(2, value_bank([P, PACK, P]))
         quantize_front_values(1)
         y23 = quantize("y23", y_late[:], on_window(2, CODES_BYTES, [P, HALF], U32, "y23_codes")[:])

from contextlib import ExitStack

import concourse.mybir as mybir
from concourse.masks import make_identity

F32 = mybir.dt.float32
BF16 = mybir.dt.bfloat16
I32 = mybir.dt.int32
U32 = mybir.dt.uint32
U16 = mybir.dt.uint16
U8 = mybir.dt.uint8
FP8X4 = mybir.dt.float8_e4m3fn_x4

P = 128
PACK = 4
SLOTS = 512
TOKENS = 2048
DISTANCES = 1024
QUERIES = 512
VALUES = 512
BANK = 512
Q_BLOCKS = QUERIES // P
V_BLOCKS = VALUES // P
HALF = 256
GROUPED = P * PACK
LIST_GROUP = 16
C_FIRST_ROW = 4
WINDOW_BYTES = 4 * TOKENS
K_BYTES_AT, C_BYTES_AT, K_WORDS_AT = V_BLOCKS, V_BLOCKS + 1, V_BLOCKS + 2
CODES_BYTES = 4 * HALF
VECTOR_SLOTS = 288

FLOPS = 3 * 2 * 512 * 512 * 512


def tile_attend_at_txl_topk_kernel(tc, uT, pT, k_words, k_scales, c_words, c_scales, vT, ls, us, offs, offs2, out):
    nc = tc.nc
    with ExitStack() as ctx:
        keep = ctx.enter_context(tc.tile_pool(name="keep", bufs=1))
        windows = ctx.enter_context(tc.tile_pool(name="values", bufs=1))
        psum = ctx.enter_context(tc.psum_pool(name="psum", bufs=1))

        def on_window(window, start, shape, dtype, name):
            return windows.tile(shape, dtype, name=name, align_bytes=64, offset=window * WINDOW_BYTES + start)

        tok_list = keep.tile([P, SLOTS // LIST_GROUP], U16, name="tok_list")
        dist_list = keep.tile([P, SLOTS // LIST_GROUP], U16, name="dist_list")
        c_word_pool = keep.tile([P, DISTANCES], I32, name="c_word_pool")
        k_word_pool = on_window(K_WORDS_AT, 0, [P, TOKENS], I32, "k_word_pool")
        c_byte_pool = on_window(C_BYTES_AT, 0, [P, DISTANCES // 4], I32, "c_byte_pool")
        k_byte_pool = on_window(K_BYTES_AT, 0, [P, TOKENS // 4], I32, "k_byte_pool")
        u_raw = keep.tile([P, PACK, QUERIES], F32, name="u_raw")
        p_raw = keep.tile([P, PACK, QUERIES], F32, name="p_raw")
        v_pool = [on_window(b, 0, [P, TOKENS], F32, "v_pool%d" % b) for b in range(V_BLOCKS)]
        ls_rows = keep.tile([P, P], F32, name="ls_rows")
        us_cols = keep.tile([P, PACK], F32, name="us_cols")
        ident = keep.tile([P, P], F32, name="ident")

        nc.gpsimd.memset(k_byte_pool[:], 0)
        nc.gpsimd.memset(c_byte_pool[:], 0)
        nc.gpsimd.memset(ls_rows[:], 0.0)
        make_identity(nc, ident[:])

        def words_of(x):
            return x[0].rearrange("p n t -> p (n t)").bitcast(I32)

        def load_position_rows(rows_in_quadrant):
            for r in rows_in_quadrant:
                nc.sync.dma_start(c_byte_pool[C_FIRST_ROW + r : P : 32, :], c_scales[0].bitcast(I32)[r:16:4, :])

        nc.sync.dma_start(c_word_pool[:], words_of(c_words))
        nc.sync.dma_start(tok_list[:], offs)
        nc.sync.dma_start(dist_list[:], offs2)
        nc.sync.dma_start(k_byte_pool[0:P:8, :], k_scales[0].bitcast(I32))
        nc.sync.dma_start(p_raw[:], pT[0].rearrange("(p t) q -> p t q", t=PACK))
        load_position_rows(range(4))
        nc.sync.dma_start(us_cols[:], us[0].rearrange("(p t) o -> p (t o)", t=PACK))
        nc.sync.dma_start(u_raw[:], uT[0].rearrange("(p t) q -> p t q", t=PACK))
        nc.sync.dma_start(k_word_pool[:], words_of(k_words))
        nc.gpsimd.dma_start(ls_rows[0:Q_BLOCKS, :], ls[0].rearrange("o (b m) -> (o b) m", m=P))

        k_picked = keep.tile([P, SLOTS], U8, name="k_picked", align_bytes=64)
        k_plane = keep.tile([P, SLOTS // 4], I32, name="k_plane", align_bytes=64)
        nc.vector.tensor_copy(k_picked[:], k_byte_pool[:].bitcast(U8).indirect(tok_list[:]))
        nc.vector.tensor_copy(k_plane[:], k_picked[:].bitcast(I32))
        for r in (1, 2, 3):
            nc.sync.dma_start(k_plane[r:P:32, :], k_picked[:].bitcast(I32)[8 * r : P : 32, :])
        k_bytes = k_plane[:].bitcast(U8)
        for b in range(V_BLOCKS):
            nc.sync.dma_start(v_pool[b][:], vT[b * P : (b + 1) * P, :])

        c_codes = on_window(K_BYTES_AT, 0, [P, SLOTS], U32, "c_codes")
        c_picked = keep.tile([P, SLOTS], U8, name="c_picked", align_bytes=64)
        k_codes = keep.tile([P, SLOTS], U32, name="k_codes", align_bytes=64)
        nc.vector.tensor_copy(c_codes[:], c_word_pool[:].bitcast(U32).indirect(dist_list[:]))
        nc.vector.tensor_copy(c_picked[:], c_byte_pool[:].bitcast(U8).indirect(dist_list[:]))
        c_bytes = c_picked[C_FIRST_ROW:P, :]

        def interleave(grouped, raw):
            src = raw.rearrange("p t (c i) -> p c t i", i=4)
            nc.scalar.copy(grouped.rearrange("p (c i t) -> p c t i", i=4, t=PACK), src)

        def code_tile(name, width):
            return keep.tile([P, width], U32, name=name + "_codes", align_bytes=64)

        def quantize(name, grouped, codes):
            scales = keep.tile([P, codes.shape[1]], U8, name=name + "_scales", align_bytes=64)
            nc.vector.quantize_mx(out=codes.bitcast(FP8X4), scales=scales[:], in_=grouped)
            return codes, scales

        def turn_bank(shape):
            return psum.tile(shape, F32, name="turn", bufs=2)

        us_turn = turn_bank([P, PACK, P])
        for t in range(PACK):
            nc.tensor.transpose(us_turn[:, t, :], us_cols[:, t : t + 1].to_broadcast([P, P]), ident[:])
        us_rows = keep.tile([P, 2, P, 2], F32, name="us_rows")
        nc.scalar.copy(us_rows[:], us_turn[:].rearrange("m (u j) p -> m u p j", j=2))

        ls_turn = turn_bank([P, PACK, P])
        nc.tensor.transpose(ls_turn[:, 0, :], ls_rows[:], ident[:])

        halves = range(2)
        half_cols = [slice(HALF * h, HALF * (h + 1)) for h in halves]
        u_grouped = [keep.tile([P, 2 * GROUPED], BF16, name="u_grouped%d" % h, align_bytes=64) for h in halves]
        p_grouped = [keep.tile([P, 2 * GROUPED], BF16, name="p_grouped%d" % h, align_bytes=64) for h in halves]
        score_banks = [psum.tile([P, BANK], F32, name="score%d" % i) for i in range(Q_BLOCKS)]

        def score_pass(acc, qb, queries_mx, codes, scale_rows, start, stop):
            cols = slice(qb % 2 * P, (qb % 2 + 1) * P)
            nc.tensor.matmul_mx(
                out=acc, lhsT=queries_mx[0][:, cols].bitcast(FP8X4), lhsT_scale=queries_mx[1][:, cols],
                rhs=codes.bitcast(FP8X4), rhs_scale=scale_rows, start=start, stop=stop,
            )

        def early_scores(qb, h):
            return score_banks[h][:, half_cols[qb]]

        for h in halves:
            interleave(p_grouped[h][:], p_raw[:, :, half_cols[h]])
        p0 = quantize("p0", p_grouped[0][:], on_window(C_BYTES_AT, 0, [P, HALF], U32, "p0_codes")[:])
        for qb in (0, 1):
            for h in halves:
                slots = half_cols[h]
                score_pass(early_scores(qb, h), qb, p0, c_codes[:, slots], c_bytes[:, slots], qb == 0, False)
        p1 = quantize("p1", p_grouped[1][:], code_tile("p1", HALF)[:])
        for qb in (2, 3):
            score_pass(score_banks[qb][:], qb, p1, c_codes[:], c_bytes, True, False)

        for h in halves:
            interleave(u_grouped[h][:], u_raw[:, :, half_cols[h]])
        neg_ls = keep.tile([P, Q_BLOCKS], F32, name="neg_ls", tag="u_raw")
        nc.scalar.mul(neg_ls[:], ls_turn[:, 0, 0:Q_BLOCKS], -1.0)
        u0 = quantize("u0", u_grouped[0][:], code_tile("u0", HALF)[:])
        for h in halves:
            slots = half_cols[h]
            entries = tok_list[:, slots.start // LIST_GROUP : slots.stop // LIST_GROUP]
            nc.vector.tensor_copy(k_codes[:, slots], k_word_pool[:].bitcast(U32).indirect(entries))
            for qb in (0, 1):
                score_pass(early_scores(qb, h), qb, u0, k_codes[:, slots], k_bytes[:, slots], False, qb == 1)
        u1 = quantize("u1", u_grouped[1][:], on_window(K_WORDS_AT, 0, [P, HALF], U32, "u1_codes")[:])
        for qb in (2, 3):
            score_pass(score_banks[qb][:], qb, u1, k_codes[:], k_bytes, False, True)

        weight_tile = keep.tile([P, Q_BLOCKS, PACK, P], F32, name="weights")
        weights = [weight_tile[:, qb] for qb in range(Q_BLOCKS)]

        def exponential(qb, laid, read):
            nc.scalar.activation(laid, read, mybir.ActivationFunctionType.Exp, bias=neg_ls[:, qb : qb + 1])

        def laid_by_pairs(qb):
            return weights[qb].rearrange("q t p -> q (t p)").rearrange("q (u p j) -> q u p j", u=2, j=2)

        def read_by_pairs(scores):
            return scores.rearrange("q (p u j) -> q u p j", u=2, j=2)

        def read_by_places(scores):
            return scores.rearrange("q (p t) -> q t p", t=PACK)

        for h in halves:
            p_range = slice(HALF // PACK * h, HALF // PACK * (h + 1))
            exponential(0, laid_by_pairs(0)[:, :, p_range, :], read_by_pairs(early_scores(0, h)))
            exponential(1, weights[1][:, :, p_range], read_by_places(early_scores(1, h)))
        exponential(2, laid_by_pairs(2), read_by_pairs(score_banks[2][:]))
        for u in range(2):
            places = slice(2 * u, 2 * u + 2)
            exponential(3, weights[3][:, places, :], read_by_places(score_banks[3][:])[:, places, :])

        us_wide = us_cols[:].unsqueeze(1).to_broadcast([P, P, PACK])
        picked = [keep.tile([P, SLOTS], BF16, name="picked%d" % b) for b in range(V_BLOCKS)]

        def as_pairs(grouped):
            return grouped.bitcast(F32).rearrange("p (c u) -> p c u", u=2)

        def scale_on_vector(qb, grouped):
            turned = turn_bank([P, PACK, P])
            for t in range(PACK):
                nc.tensor.transpose(turned[:, t, :], weights[qb][:, t, :], ident[:])
            nc.vector.tensor_tensor(
                grouped.rearrange("p (q t) -> p q t", t=PACK), turned[:].rearrange("p t q -> p q t"), us_wide,
                mybir.AluOpType.mult,
            )

        def scale_on_scalar(qb, grouped):
            y_pairs = keep.tile([P, 2, P, 2], BF16, name="y_pairs", tag="scaled0")
            banks = [turn_bank([P, 2, P]), psum.tile([P, 2, P], F32, name="score2")]
            for t in range(PACK):
                nc.tensor.transpose(banks[t // 2][:, t % 2, :], weights[qb][:, t, :], ident[:])
            for t in range(PACK):
                nc.scalar.activation(
                    y_pairs[:, t // 2, :, t % 2], banks[t // 2][:, t % 2, :],
                    mybir.ActivationFunctionType.Copy, scale=us_cols[:, t : t + 1],
                )
            nc.scalar.copy(
                as_pairs(grouped),
                y_pairs[:].rearrange("p u q j -> p (u q j)").bitcast(F32).rearrange("p (u q) -> p q u", u=2),
            )

        def scale_on_gpsimd(qb, grouped, bank):
            scaled = keep.tile([P, SLOTS], BF16, name="scaled%d" % qb)
            nc.gpsimd.tensor_tensor(
                scaled[:], weights[qb].rearrange("q t p -> q (t p)"), us_rows[:].rearrange("q u p j -> q (u p j)"),
                mybir.AluOpType.mult,
            )
            pairs = scaled[:].bitcast(F32)
            turned = psum.tile([P, PACK, P], F32, name=bank)
            for u in range(2):
                nc.tensor.transpose(turned[:, u, :], pairs[:, u * P : (u + 1) * P], ident[:])
            nc.scalar.copy(as_pairs(grouped), turned[:, 0:2, :].rearrange("p u q -> p q u"))

        def gather_values(b, split=SLOTS):
            column = split // LIST_GROUP
            nc.vector.tensor_copy(picked[b][:, 0:split], v_pool[b][:].indirect(tok_list[:, 0:column]))
            if split < SLOTS:
                window = v_pool[b][:].indirect(tok_list[:, column : SLOTS // LIST_GROUP])
                nc.scalar.activation(picked[b][:, split:SLOTS], window, mybir.ActivationFunctionType.Copy)

        def value_bank(shape):
            return psum.tile(shape, F32, name="v_turn", bufs=2)

        def turn_values(b, turned):
            pairs = picked[b][:].bitcast(F32)
            for u in range(2):
                nc.tensor.transpose(turned[:, u, :], pairs[:, u : 2 * P : 2], ident[:])
            nc.scalar.copy(as_pairs(v_grouped[b]), turned[:, 0:2, :].rearrange("p u e -> p e u"))

        out_rows = out[0].rearrange("(b q) e -> q b e", q=P)

        def product(acc, qb, v_mx):
            nc.tensor.matmul_mx(
                out=acc, lhsT=y_mx[qb][0].bitcast(FP8X4), lhsT_scale=y_mx[qb][1],
                rhs=v_mx[0].bitcast(FP8X4), rhs_scale=v_mx[1][:], start=True, stop=True,
            )

        def products_out(v_mx, first_feature, q_blocks, acc, staged):
            width = v_mx[0].shape[1]
            for i, qb in enumerate(q_blocks):
                product(acc[:, i * width : (i + 1) * width], qb, v_mx)
            nc.scalar.copy(staged[:], acc[:, 0 : len(q_blocks) * width])
            nc.sync.dma_start(
                out_rows[:, q_blocks[0] : q_blocks[-1] + 1, first_feature : first_feature + width],
                staged[:].rearrange("q (b e) -> q b e", e=width),
            )

        v_front = keep.tile([P, 2, GROUPED], BF16, name="v_front", align_bytes=64)
        v_back = keep.tile([P, 2, GROUPED], BF16, name="v_back", align_bytes=64)
        v_grouped = [v_front[:, 0], v_front[:, 1], v_back[:, 0], v_back[:, 1]]
        first, second = slice(0, GROUPED), slice(GROUPED, 2 * GROUPED)

        gather_values(0)
        y_late = keep.tile([P, 2 * GROUPED], BF16, name="y_late", align_bytes=64)
        y_early = on_window(0, 0, [P, 2 * GROUPED], BF16, "y_early")
        scale_on_vector(1, y_early[:, second])
        turn_values(0, psum.tile([P, PACK, P], F32, name="score1"))
        scale_on_gpsimd(0, y_early[:, first], "score0")
        scale_on_scalar(3, y_late[:, second])
        scale_on_gpsimd(2, y_late[:, first], "score3")
        gather_values(1)
        turn_values(1, value_bank([P, PACK, P]))
        y01 = quantize("y01", y_early[:], on_window(1, 0, [P, HALF], U32, "y01_codes")[:])
        v01_codes = on_window(2, -CODES_BYTES // 2, [P, 2 * P], U32, "v01_codes")
        v01_scales = keep.tile([P, 2 * P], U8, name="v01_scales", align_bytes=64)
        v01 = (v01_codes[:], v01_scales)

        def quantize_front_values(b):
            cols = slice(b * P, (b + 1) * P)
            nc.vector.quantize_mx(out=v01_codes[:, cols].bitcast(FP8X4), scales=v01_scales[:, cols], in_=v_grouped[b])

        quantize_front_values(0)
        gather_values(2, 384)
        turn_values(2, value_bank([P, PACK, P]))
        quantize_front_values(1)
        y23 = quantize("y23", y_late[:], on_window(2, CODES_BYTES, [P, HALF], U32, "y23_codes")[:])
        y_mx = [(y[0][:, i * P : (i + 1) * P], y[1][:, i * P : (i + 1) * P]) for y in (y01, y23) for i in range(2)]

        front_banks = [turn_bank([P, BANK]), turn_bank([P, BANK])]
        for qb in range(Q_BLOCKS):
            product(front_banks[qb // 2][:, qb % 2 * HALF : (qb % 2 + 1) * HALF], qb, v01)
        gather_values(3, VECTOR_SLOTS)
        v2 = quantize("v2", v_grouped[2], on_window(3, 0, [P, P], U32, "v2_codes")[:])
        front = on_window(3, CODES_BYTES, [P, Q_BLOCKS, HALF], F32, "front")
        nc.scalar.copy(front[:, 0:2, :], front_banks[0][:].rearrange("q (b e) -> q b e", b=2))
        nc.sync.dma_start(out_rows[:, 0:2, 0:HALF], front[:, 0:2, :])
        nc.vector.tensor_copy(front[:, 2:4, :], front_banks[1][:].rearrange("q (b e) -> q b e", b=2))
        nc.sync.dma_start(out_rows[:, 2:4, 0:HALF], front[:, 2:4, :])
        turn_values(3, value_bank([P, PACK, P]))
        v3 = quantize("v3", v_grouped[3], code_tile("v3", P)[:])

        products_out(v2, 2 * P, (0, 1), psum.tile([P, BANK], F32, name="score2"), keep.tile([P, 2 * P], F32, name="third0"))
        products_out(v2, 2 * P, (2, 3), value_bank([P, BANK]), keep.tile([P, 2 * P], F32, name="third1"))

        last_staged = [keep.tile([P, 2, P], F32, name="last%d" % h) for h in halves]
        for qb in range(Q_BLOCKS):
            if qb < Q_BLOCKS - 1:
                acc = psum.tile([P, BANK], F32, name="score%d" % ((qb - 1) % Q_BLOCKS))
            else:
                acc = turn_bank([P, BANK])
            product(acc[:, 0:P], qb, v3)
            (nc.vector.tensor_copy, nc.scalar.copy)[qb // 2](last_staged[qb // 2][:, qb % 2, :], acc[:, 0:P])
        nc.sync.dma_start(out_rows[:, 0:2, 3 * P : 4 * P], last_staged[0][:])
        nc.scalar.dma_start(out_rows[:, 2:4, 3 * P : 4 * P], last_staged[1][:])
